import numpy as np
import ml_dtypes


def mxq(x, axis, fmt="e4m3"):
    dtype, down = {"e4m3": (ml_dtypes.float8_e4m3fn, 7), "e5m2": (ml_dtypes.float8_e5m2, 14)}[fmt]
    v = np.moveaxis(np.asarray(x, np.float32).astype(ml_dtypes.bfloat16).astype(np.float64), axis, -1)
    blocks = v.reshape(v.shape[:-1] + (-1, 32))
    amax = np.abs(blocks).max(-1, keepdims=True)
    byte = np.maximum(np.where(amax > 0, np.frexp(amax)[1] - 1 + 127, 0) - down, 1)
    scale = np.exp2(byte - 127.0)
    codes = (blocks / scale).astype(np.float32).astype(dtype).astype(np.float64)
    return np.moveaxis((codes * scale).reshape(v.shape), -1, axis)


WIDE = False


def mx_kscale(k):
    if not WIDE:
        return np.ones(k)
    levels = np.array([10, -10, 5, -5, 0])
    if k % 512:
        return np.exp2(np.random.permutation(np.resize(levels, k // 32))).repeat(32)
    a = np.empty((k // 512, 16))
    for p in range(k // 512):
        a[p, :8] = np.random.permutation(np.resize(levels, 8))
        for g in range(8):
            far = levels[np.abs(levels - a[p, g]) >= 10]
            a[p, g + 8] = far[np.random.randint(len(far))]
    return np.exp2(a.ravel()).repeat(32)


def f64(x):
    return np.asarray(x).astype(np.float64)


def striped(idx):
    return np.tile(np.asarray(idx).reshape(-1, 16).T, (8, 1)).astype(np.uint16)


def unstriped(offs):
    return offs[:16].T.reshape(-1).astype(np.int64)


E2M1 = np.array([0.0, 0.5, 1.0, 1.5, 2.0, 3.0, 4.0, 6.0, -0.0, -0.5, -1.0, -1.5, -2.0, -3.0, -4.0, -6.0])


def pack_weight(w, fmt):
    k, n = w.shape
    w = f64(np.asarray(w, np.float32).astype(ml_dtypes.bfloat16)).reshape(k // 32, 32, n)
    amax = np.abs(w).max(1)
    if fmt == "e4m3":
        byte = np.frexp(amax)[1] - 1 + 127 - 7
    else:
        mant, ex = np.frexp(amax / 6.0)
        byte = np.where(mant > 0.5, ex, ex - 1) + 127
    byte = np.clip(np.where(amax > 0, byte, 1), 1, 254)
    scaled = (w * np.exp2(127.0 - byte)[:, None, :]).reshape(k, n).astype(np.float32)
    by_word = np.ascontiguousarray(scaled.reshape(k // 512, 128, 4, n).transpose(0, 1, 3, 2))
    if fmt == "e4m3":
        words = by_word.astype(ml_dtypes.float8_e4m3fn).view(np.uint8)
    else:
        c = by_word.astype(ml_dtypes.float4_e2m1fn).view(np.uint8) & 0xF
        words = (c[..., 0::2] | (c[..., 1::2] << 4)).reshape(k // 512, 128, 2 * n)
    return np.ascontiguousarray(words), np.ascontiguousarray(byte.astype(np.uint8).reshape(k // 512, 16, n))


def unpack_weight(words, scales, fmt):
    g, _, n = scales.shape
    words = np.ascontiguousarray(words).reshape(g, 128, n, -1)
    if fmt == "e4m3":
        vals = words.view(ml_dtypes.float8_e4m3fn).astype(np.float64)
    else:
        nib = np.empty((g, 128, n, 4), np.uint8)
        nib[..., 0::2] = words & 0xF
        nib[..., 1::2] = words >> 4
        vals = E2M1[nib]
    vals = vals * np.repeat(np.exp2(scales.astype(np.float64) - 127.0), 8, axis=1)[..., None]
    return vals.transpose(0, 1, 3, 2).reshape(g * 512, n)


def bf(x):
    return np.asarray(x, np.float32).astype(ml_dtypes.bfloat16)


def planes(Y):
    r, m = Y.shape
    b = f64(bf(Y)).reshape(r // 32, 32, m)
    amax = np.abs(b).max(1)
    byte = np.clip(np.where(amax > 0, np.frexp(amax)[1] - 1 + 127 - 7, 1), 1, 254)
    codes = (b * np.exp2(127.0 - byte)[:, None, :]).reshape(r, m).astype(np.float32).astype(ml_dtypes.float8_e4m3fn).view(np.uint8)
    words = codes.reshape(r // 512, 128, 4, m).transpose(0, 1, 3, 2)
    return np.ascontiguousarray(words), np.ascontiguousarray(byte.astype(np.uint8).reshape(r // 512, 16, m))


B, N, T, D, NQ = 1, 512, 2048, 512, 512


def setup_inputs():
    n = np.random.standard_normal
    idx = np.sort(np.random.permutation(T)[:B * N].reshape(B, N), axis=1).reshape(-1)
    s = mx_kscale(D)[:, None]
    kp = pack_weight(n((D, T)) / s, "e4m3")
    return {
        "qT": (n((B, D, NQ)) * s * (1.00 / np.sqrt(D))).astype(np.float32),
        "k_words": kp[0],
        "k_scales": kp[1],
        "dk": np.tile(np.random.uniform(0.1, 1.0, 2048), (128, 1)).astype(np.float32),
        "dc": (np.random.uniform(0.1, 1.0, (B, 1, NQ))).astype(np.float32),
        "offs": striped(idx),
    }


def reference(qT, k_words, k_scales, dk, dc, offs):
    idx = unstriped(offs)
    pick = lambda x, which: x[:, which].reshape(x.shape[0], B, -1).transpose(1, 0, 2)
    k = unpack_weight(k_words, k_scales, "e4m3")
    kg = pick(k, idx)
    qq = mxq(f64(qT), 1, "e4m3")
    a = kg.transpose(0, 2, 1) @ qq
    y = a * pick(f64(dk), idx)[:, :1, :].transpose(0, 2, 1) * f64(dc)
    Y = y[0]
    words, scales = planes(Y)
    return Y, words, scales

@@ -1,0 +1,157 @@
+from contextlib import ExitStack
+
+import concourse.mybir as mybir
+from concourse.masks import make_identity
+
+F32 = mybir.dt.float32
+BF16 = mybir.dt.bfloat16
+I32 = mybir.dt.int32
+U32 = mybir.dt.uint32
+U16 = mybir.dt.uint16
+U8 = mybir.dt.uint8
+FP8X4 = mybir.dt.float8_e4m3fn_x4
+MULT = mybir.AluOpType.mult
+
+P = 128
+PACK = 4
+T = 2048
+N = 512
+D = 512
+NQ = 512
+BANK = 512
+CHUNKS = [128, 128, 128, 128]
+LOADS = [256, 256]
+BEFORE_KEYS = 1
+VECTOR_WEAVES = (3,)
+
+FLOPS = 2 * N * D * NQ
+BYTES = 4 * D * NQ + D * T + 16 * T + 4 * T + 4 * NQ + 2 * P * N // 16 + 4 * N * NQ + N * NQ + 16 * NQ
+
+
+def weave(copy, dst, src):
+    copy(
+        out=dst.rearrange("p (c i) t -> p c t i", i=4),
+        in_=src.rearrange("p t (c i) -> p c t i", i=4),
+    )
+
+
+def tile_attend_plw_decay_srt_kernel(tc, qT, k_words, k_scales, dk, dc, offs, out_0, out_1, out_2):
+    nc = tc.nc
+    starts = [sum(CHUNKS[:c]) for c in range(len(CHUNKS))]
+    cols = [slice(s, s + w) for s, w in zip(starts, CHUNKS)]
+    load_starts = [sum(LOADS[:g]) for g in range(len(LOADS))]
+    load_cols = [slice(s, s + w) for s, w in zip(load_starts, LOADS)]
+    with ExitStack() as ctx:
+        sb = ctx.enter_context(tc.tile_pool(name="sb", bufs=1))
+        ps = ctx.enter_context(tc.psum_pool(name="ps", bufs=1))
+
+        offsets = sb.tile([P, N // 16], U16, name="offsets")
+        dk_pool = sb.tile([P, T], F32, name="dk_pool")
+        word_pool = sb.tile([P, T], U32, name="word_pool")
+        scale_pool = sb.tile([P, T], U8, name="scale_pool")
+        dc_quads = sb.tile([P, PACK], F32, name="dc_quads")
+        ident = sb.tile([P, P], F32, name="ident")
+        q_raw = [sb.tile([P, PACK, w], F32, name=f"q_raw{c}") for c, w in enumerate(LOADS)]
+
+        nc.vector.memset(scale_pool[:].bitcast(I32), 0)
+        nc.vector.memset(dk_pool[0 : P - 1, :].bitcast(I32), 0)
+        make_identity(nc, ident[:])
+
+        q_rows = qT[0].rearrange("(p t) q -> p t q", t=PACK)
+        nc.sync.dma_start(offsets[:], offs)
+        nc.sync.dma_start(dk_pool[P - 1 : P, :], dk[0:1, :])
+        for c in range(BEFORE_KEYS):
+            nc.sync.dma_start(q_raw[c][:], q_rows[:, :, load_cols[c]])
+        nc.sync.dma_start(word_pool[:].bitcast(I32), k_words[0].rearrange("p n r -> p (n r)").bitcast(I32))
+        for quad in range(4):
+            nc.scalar.dma_start(
+                scale_pool[32 * quad : 32 * quad + 4, :].bitcast(I32),
+                k_scales[0, 4 * quad : 4 * quad + 4, :].bitcast(I32),
+            )
+        nc.scalar.dma_start(dc_quads[:], dc[0, 0].rearrange("(p u) -> p u", u=PACK))
+        for c in range(BEFORE_KEYS, len(LOADS)):
+            nc.sync.dma_start(q_raw[c][:], q_rows[:, :, load_cols[c]])
+
+        dk_listed = sb.tile([P, N], F32, name="dk_listed")
+        nc.vector.tensor_copy(dk_listed[:], dk_pool[:].indirect(offsets[:]))
+        scale_listed = sb.tile([P, N], U8, name="scale_listed")
+        nc.vector.tensor_copy(scale_listed[:], scale_pool[:].indirect(offsets[:]))
+        k_codes = sb.tile([P, N], U32, name="k_codes", align_bytes=64)
+        nc.vector.tensor_copy(
+            k_codes[:].rearrange("p (t m) -> p m t", t=PACK), word_pool[:].indirect(offsets[:])
+        )
+        k_scale = sb.tile([P, N], U8, name="k_scale", align_bytes=64)
+        nc.vector.tensor_copy(
+            k_scale[:].rearrange("p (t m) -> p t m", t=PACK),
+            scale_listed[:].rearrange("p (m t) -> p t m", t=PACK),
+        )
+
+        dc_bank = ps.tile([P, PACK, P], F32, name="dc_bank")
+        for u in range(PACK):
+            nc.tensor.transpose(dc_bank[:, u, :], dc_quads[:, u : u + 1].to_broadcast([P, P]), ident[:])
+        dc_rows = sb.tile([P, NQ], F32, name="dc_rows")
+        nc.scalar.copy(dc_rows[:].rearrange("p (n u) -> p n u", u=PACK), dc_bank[:].rearrange("p u n -> p n u"))
+
+        dk_bank = ps.tile([P, PACK, P], F32, name="dk_bank")
+        dk_dealt = dk_listed[:].rearrange("p (m t) -> p t m", t=PACK)
+        for t in range(PACK):
+            nc.tensor.transpose(dk_bank[:, t, :], dk_dealt[:, t, :], ident[:])
+        dk_slots = sb.tile([P, PACK], F32, name="dk_slots")
+        nc.scalar.copy(dk_slots[:], dk_bank[:, :, P - 1])
+
+        q_codes, q_scale = [], []
+        for c, w in enumerate(LOADS):
+            q_woven = sb.tile([P, w, PACK], BF16, name=f"q_woven{c}", align_bytes=64)
+            weave(nc.scalar.copy, q_woven[:], q_raw[c][:])
+            q_codes.append(sb.tile([P, w], U32, name=f"q_codes{c}", align_bytes=64))
+            q_scale.append(sb.tile([P, w], U8, name=f"q_scale{c}", align_bytes=64))
+            nc.vector.quantize_mx(
+                out=q_codes[c][:].bitcast(FP8X4),
+                scales=q_scale[c][:],
+                in_=q_woven[:].rearrange("p w t -> p (w t)"),
+            )
+
+        y_rows = out_0.rearrange("(p t) q -> p t q", t=PACK)
+        y_words = out_1[0].rearrange("p q u -> p (q u)").bitcast(I32)
+        y_scale = sb.tile([P, NQ], U8, name="y_scale", align_bytes=64)
+        for c, w in enumerate(CHUNKS):
+            g = max(i for i, s in enumerate(load_starts) if s <= starts[c])
+            inside = slice(starts[c] - load_starts[g], starts[c] - load_starts[g] + w)
+            per_bank = BANK // w
+            banks = [ps.tile([P, per_bank, w], F32, name=f"score{c}_{b}") for b in range(PACK // per_bank)]
+            y = sb.tile([P, PACK, w], F32, name=f"y{c}")
+            for t in range(PACK):
+                nc.tensor.matmul_mx(
+                    out=banks[t // per_bank][:, t % per_bank, :],
+                    lhsT=k_codes[:, t * P : (t + 1) * P].bitcast(FP8X4),
+                    lhsT_scale=k_scale[:, t * P : (t + 1) * P],
+                    rhs=q_codes[g][:, inside].bitcast(FP8X4),
+                    rhs_scale=q_scale[g][:, inside],
+                    start=True,
+                    stop=True,
+                )
+            for t in range(PACK):
+                nc.vector.scalar_tensor_tensor(
+                    out=y[:, t, :],
+                    in0=banks[t // per_bank][:, t % per_bank, :],
+                    scalar=dk_slots[:, t : t + 1],
+                    in1=dc_rows[:, cols[c]],
+                    op0=MULT,
+                    op1=MULT,
+                )
+            nc.sync.dma_start(y_rows[:, :, cols[c]], y[:])
+            y_woven = sb.tile([P, w, PACK], BF16, name=f"y_woven{c}", align_bytes=64)
+            weave(nc.vector.tensor_copy if c in VECTOR_WEAVES else nc.scalar.copy, y_woven[:], y[:])
+            y_codes = sb.tile([P, w], U32, name=f"y_codes{c}", align_bytes=64)
+            nc.vector.quantize_mx(
+                out=y_codes[:].bitcast(FP8X4),
+                scales=y_scale[:, cols[c]],
+                in_=y_woven[:].rearrange("p w t -> p (w t)"),
+            )
+            nc.sync.dma_start(y_words[:, cols[c]], y_codes[:].bitcast(I32))
+        for quad in range(4):
+            queue = nc.scalar if quad % 2 == 0 else nc.sync
+            queue.dma_start(
+                out_2[0, 4 * quad : 4 * quad + 4, :].bitcast(I32),
+                y_scale[32 * quad : 32 * quad + 4, :].bitcast(I32),
+            )

@@ -18,11 +18,9 @@ T = 2048
 N = 512
 D = 512
 NQ = 512
-BANK = 512
-CHUNKS = [128, 128, 128, 128]
-LOADS = [256, 256]
-BEFORE_KEYS = 1
-VECTOR_WEAVES = (3,)
+W = 128
+CHUNKS = NQ // W
+SPLIT = 1152
 
 FLOPS = 2 * N * D * NQ
 BYTES = 4 * D * NQ + D * T + 16 * T + 4 * T + 4 * NQ + 2 * P * N // 16 + 4 * N * NQ + N * NQ + 16 * NQ
@@ -37,43 +35,50 @@ def weave(copy, dst, src):
 
 def tile_attend_plw_decay_srt_kernel(tc, qT, k_words, k_scales, dk, dc, offs, out_0, out_1, out_2):
     nc = tc.nc
-    starts = [sum(CHUNKS[:c]) for c in range(len(CHUNKS))]
-    cols = [slice(s, s + w) for s, w in zip(starts, CHUNKS)]
-    load_starts = [sum(LOADS[:g]) for g in range(len(LOADS))]
-    load_cols = [slice(s, s + w) for s, w in zip(load_starts, LOADS)]
+    cols = [slice(c * W, (c + 1) * W) for c in range(CHUNKS)]
     with ExitStack() as ctx:
         sb = ctx.enter_context(tc.tile_pool(name="sb", bufs=1))
+        reused = ctx.enter_context(tc.tile_pool(name="reused", bufs=1))
         ps = ctx.enter_context(tc.psum_pool(name="ps", bufs=1))
 
         offsets = sb.tile([P, N // 16], U16, name="offsets")
-        dk_pool = sb.tile([P, T], F32, name="dk_pool")
+        dk_pool = reused.tile([P, T], F32, name="dk_pool", offset=0)
         word_pool = sb.tile([P, T], U32, name="word_pool")
         scale_pool = sb.tile([P, T], U8, name="scale_pool")
-        dc_quads = sb.tile([P, PACK], F32, name="dc_quads")
         ident = sb.tile([P, P], F32, name="ident")
-        q_raw = [sb.tile([P, PACK, w], F32, name=f"q_raw{c}") for c, w in enumerate(LOADS)]
+        q_first = sb.tile([P, PACK, W], F32, name="q_first")
 
-        nc.vector.memset(scale_pool[:].bitcast(I32), 0)
-        nc.vector.memset(dk_pool[0 : P - 1, :].bitcast(I32), 0)
+        scale_zero = scale_pool[:].bitcast(I32)
+        nc.vector.memset(scale_zero[:, 0 : T // 8], 0)
+        nc.gpsimd.memset(scale_zero[:, T // 8 : T // 4], 0)
+        dk_zero = dk_pool[0 : P - 1, :].bitcast(I32)
+        nc.vector.memset(dk_zero[:, 0 : SPLIT - 1], 0)
+        nc.vector.memset(dk_zero[:, SPLIT - 1 : SPLIT], 0)
+        nc.gpsimd.memset(dk_zero[:, SPLIT:T], 0)
         make_identity(nc, ident[:])
 
         q_rows = qT[0].rearrange("(p t) q -> p t q", t=PACK)
         nc.sync.dma_start(offsets[:], offs)
         nc.sync.dma_start(dk_pool[P - 1 : P, :], dk[0:1, :])
-        for c in range(BEFORE_KEYS):
-            nc.sync.dma_start(q_raw[c][:], q_rows[:, :, load_cols[c]])
-        nc.sync.dma_start(word_pool[:].bitcast(I32), k_words[0].rearrange("p n r -> p (n r)").bitcast(I32))
+        nc.sync.dma_start(q_first[:], q_rows[:, :, cols[0]])
         for quad in range(4):
-            nc.scalar.dma_start(
+            queue = nc.scalar if quad < 2 else nc.sync
+            queue.dma_start(
                 scale_pool[32 * quad : 32 * quad + 4, :].bitcast(I32),
                 k_scales[0, 4 * quad : 4 * quad + 4, :].bitcast(I32),
             )
-        nc.scalar.dma_start(dc_quads[:], dc[0, 0].rearrange("(p u) -> p u", u=PACK))
-        for c in range(BEFORE_KEYS, len(LOADS)):
-            nc.sync.dma_start(q_raw[c][:], q_rows[:, :, load_cols[c]])
+        nc.sync.dma_start(word_pool[:].bitcast(I32), k_words[0].rearrange("p n r -> p (n r)").bitcast(I32))
 
         dk_listed = sb.tile([P, N], F32, name="dk_listed")
         nc.vector.tensor_copy(dk_listed[:], dk_pool[:].indirect(offsets[:]))
+        dc_quads = reused.tile([P, PACK], F32, name="dc_quads", offset=0)
+        nc.sync.dma_start(dc_quads[:], dc[0, 0].rearrange("(p u) -> p u", u=PACK))
+        q_raw = [q_first[:]]
+        for c in range(1, CHUNKS):
+            q_late = reused.tile([P, PACK, W], F32, name=f"q_late{c}", offset=c * PACK * W * 4)
+            nc.sync.dma_start(q_late[:], q_rows[:, :, cols[c]])
+            q_raw.append(q_late[:])
+
         scale_listed = sb.tile([P, N], U8, name="scale_listed")
         nc.vector.tensor_copy(scale_listed[:], scale_pool[:].indirect(offsets[:]))
         k_codes = sb.tile([P, N], U32, name="k_codes", align_bytes=64)
@@ -86,7 +91,7 @@ def tile_attend_plw_decay_srt_kernel(tc, qT, k_words, k_scales, dk, dc, offs, ou
             scale_listed[:].rearrange("p (m t) -> p t m", t=PACK),
         )
 
-        dc_bank = ps.tile([P, PACK, P], F32, name="dc_bank")
+        dc_bank = ps.tile([P, PACK, P], F32, name="dc_bank", tag="dc_then_last")
         for u in range(PACK):
             nc.tensor.transpose(dc_bank[:, u, :], dc_quads[:, u : u + 1].to_broadcast([P, P]), ident[:])
         dc_rows = sb.tile([P, NQ], F32, name="dc_rows")
@@ -96,15 +101,13 @@ def tile_attend_plw_decay_srt_kernel(tc, qT, k_words, k_scales, dk, dc, offs, ou
         dk_dealt = dk_listed[:].rearrange("p (m t) -> p t m", t=PACK)
         for t in range(PACK):
             nc.tensor.transpose(dk_bank[:, t, :], dk_dealt[:, t, :], ident[:])
-        dk_slots = sb.tile([P, PACK], F32, name="dk_slots")
-        nc.scalar.copy(dk_slots[:], dk_bank[:, :, P - 1])
 
         q_codes, q_scale = [], []
-        for c, w in enumerate(LOADS):
-            q_woven = sb.tile([P, w, PACK], BF16, name=f"q_woven{c}", align_bytes=64)
-            weave(nc.scalar.copy, q_woven[:], q_raw[c][:])
-            q_codes.append(sb.tile([P, w], U32, name=f"q_codes{c}", align_bytes=64))
-            q_scale.append(sb.tile([P, w], U8, name=f"q_scale{c}", align_bytes=64))
+        for c in range(CHUNKS):
+            q_woven = sb.tile([P, W, PACK], BF16, name=f"q_woven{c}", align_bytes=64)
+            weave(nc.scalar.copy, q_woven[:], q_raw[c])
+            q_codes.append(sb.tile([P, W], U32, name=f"q_codes{c}", align_bytes=64))
+            q_scale.append(sb.tile([P, W], U8, name=f"q_scale{c}", align_bytes=64))
             nc.vector.quantize_mx(
                 out=q_codes[c][:].bitcast(FP8X4),
                 scales=q_scale[c][:],
@@ -113,44 +116,50 @@ def tile_attend_plw_decay_srt_kernel(tc, qT, k_words, k_scales, dk, dc, offs, ou
 
         y_rows = out_0.rearrange("(p t) q -> p t q", t=PACK)
         y_words = out_1[0].rearrange("p q u -> p (q u)").bitcast(I32)
+        y_codes = sb.tile([P, NQ], U32, name="y_codes", align_bytes=64)
         y_scale = sb.tile([P, NQ], U8, name="y_scale", align_bytes=64)
-        for c, w in enumerate(CHUNKS):
-            g = max(i for i, s in enumerate(load_starts) if s <= starts[c])
-            inside = slice(starts[c] - load_starts[g], starts[c] - load_starts[g] + w)
-            per_bank = BANK // w
-            banks = [ps.tile([P, per_bank, w], F32, name=f"score{c}_{b}") for b in range(PACK // per_bank)]
-            y = sb.tile([P, PACK, w], F32, name=f"y{c}")
+        ys = []
+        for c in range(CHUNKS):
+            if c == 0:
+                scores = [ps.tile([P, W], F32, name=f"score0_{t}")[:] for t in range(PACK)]
+            else:
+                bank = ps.tile([P, PACK, W], F32, name=f"score{c}", tag="dc_then_last" if c == CHUNKS - 1 else f"score{c}")
+                scores = [bank[:, t, :] for t in range(PACK)]
+            y = sb.tile([P, PACK, W], F32, name=f"y{c}")
+            ys.append(y)
             for t in range(PACK):
                 nc.tensor.matmul_mx(
-                    out=banks[t // per_bank][:, t % per_bank, :],
+                    out=scores[t],
                     lhsT=k_codes[:, t * P : (t + 1) * P].bitcast(FP8X4),
                     lhsT_scale=k_scale[:, t * P : (t + 1) * P],
-                    rhs=q_codes[g][:, inside].bitcast(FP8X4),
-                    rhs_scale=q_scale[g][:, inside],
+                    rhs=q_codes[c][:].bitcast(FP8X4),
+                    rhs_scale=q_scale[c][:],
                     start=True,
                     stop=True,
                 )
             for t in range(PACK):
                 nc.vector.scalar_tensor_tensor(
                     out=y[:, t, :],
-                    in0=banks[t // per_bank][:, t % per_bank, :],
-                    scalar=dk_slots[:, t : t + 1],
+                    in0=scores[t],
+                    scalar=dk_bank[:, t, P - 1 : P],
                     in1=dc_rows[:, cols[c]],
                     op0=MULT,
                     op1=MULT,
                 )
             nc.sync.dma_start(y_rows[:, :, cols[c]], y[:])
-            y_woven = sb.tile([P, w, PACK], BF16, name=f"y_woven{c}", align_bytes=64)
-            weave(nc.vector.tensor_copy if c in VECTOR_WEAVES else nc.scalar.copy, y_woven[:], y[:])
-            y_codes = sb.tile([P, w], U32, name=f"y_codes{c}", align_bytes=64)
+            y_woven = sb.tile([P, W, PACK], BF16, name=f"y_woven{c}", align_bytes=64)
+            weave(nc.vector.tensor_copy if c == CHUNKS - 1 else nc.scalar.copy, y_woven[:], y[:])
             nc.vector.quantize_mx(
-                out=y_codes[:].bitcast(FP8X4),
+                out=y_codes[:, cols[c]].bitcast(FP8X4),
                 scales=y_scale[:, cols[c]],
                 in_=y_woven[:].rearrange("p w t -> p (w t)"),
             )
-            nc.sync.dma_start(y_words[:, cols[c]], y_codes[:].bitcast(I32))
+            if c > 0:
+                done = slice(0, 2 * W) if c == 1 else cols[c]
+                queue = nc.scalar if c == CHUNKS - 1 else nc.sync
+                queue.dma_start(y_words[:, done], y_codes[:, done].bitcast(I32))
         for quad in range(4):
-            queue = nc.scalar if quad % 2 == 0 else nc.sync
+            queue = nc.scalar if quad == 0 else nc.sync
             queue.dma_start(
                 out_2[0, 4 * quad : 4 * quad + 4, :].bitcast(I32),
                 y_scale[32 * quad : 32 * quad + 4, :].bitcast(I32),

@@ -18,7 +18,8 @@ T = 2048
 N = 512
 D = 512
 NQ = 512
-W = 128
+W = 256
+HALF = W // 2
 CHUNKS = NQ // W
 SPLIT = 1152
 
@@ -33,6 +34,10 @@ def weave(copy, dst, src):
     )
 
 
+def quantize(nc, codes, scales, woven):
+    nc.vector.quantize_mx(out=codes.bitcast(FP8X4), scales=scales, in_=woven.rearrange("p w t -> p (w t)"))
+
+
 def tile_attend_plw_decay_srt_kernel(tc, qT, k_words, k_scales, dk, dc, offs, out_0, out_1, out_2):
     nc = tc.nc
     cols = [slice(c * W, (c + 1) * W) for c in range(CHUNKS)]
@@ -42,11 +47,12 @@ def tile_attend_plw_decay_srt_kernel(tc, qT, k_words, k_scales, dk, dc, offs, ou
         ps = ctx.enter_context(tc.psum_pool(name="ps", bufs=1))
 
         offsets = sb.tile([P, N // 16], U16, name="offsets")
-        dk_pool = reused.tile([P, T], F32, name="dk_pool", offset=0)
-        word_pool = sb.tile([P, T], U32, name="word_pool")
+        dk_pool = sb.tile([P, T], F32, name="dk_pool")
+        word_pool = reused.tile([P, T], U32, name="word_pool", offset=0, align_bytes=64)
         scale_pool = sb.tile([P, T], U8, name="scale_pool")
         ident = sb.tile([P, P], F32, name="ident")
-        q_first = sb.tile([P, PACK, W], F32, name="q_first")
+        dc_quads = sb.tile([P, PACK], F32, name="dc_quads")
+        q_raw = [sb.tile([P, PACK, W], F32, name=f"q_raw{c}") for c in range(CHUNKS)]
 
         scale_zero = scale_pool[:].bitcast(I32)
         nc.vector.memset(scale_zero[:, 0 : T // 8], 0)
@@ -60,7 +66,7 @@ def tile_attend_plw_decay_srt_kernel(tc, qT, k_words, k_scales, dk, dc, offs, ou
         q_rows = qT[0].rearrange("(p t) q -> p t q", t=PACK)
         nc.sync.dma_start(offsets[:], offs)
         nc.sync.dma_start(dk_pool[P - 1 : P, :], dk[0:1, :])
-        nc.sync.dma_start(q_first[:], q_rows[:, :, cols[0]])
+        nc.sync.dma_start(dc_quads[:], dc[0, 0].rearrange("(p u) -> p u", u=PACK))
         for quad in range(4):
             queue = nc.scalar if quad < 2 else nc.sync
             queue.dma_start(
@@ -68,16 +74,11 @@ def tile_attend_plw_decay_srt_kernel(tc, qT, k_words, k_scales, dk, dc, offs, ou
                 k_scales[0, 4 * quad : 4 * quad + 4, :].bitcast(I32),
             )
         nc.sync.dma_start(word_pool[:].bitcast(I32), k_words[0].rearrange("p n r -> p (n r)").bitcast(I32))
+        for c in range(CHUNKS):
+            nc.sync.dma_start(q_raw[c][:], q_rows[:, :, cols[c]])
 
         dk_listed = sb.tile([P, N], F32, name="dk_listed")
         nc.vector.tensor_copy(dk_listed[:], dk_pool[:].indirect(offsets[:]))
-        dc_quads = reused.tile([P, PACK], F32, name="dc_quads", offset=0)
-        nc.sync.dma_start(dc_quads[:], dc[0, 0].rearrange("(p u) -> p u", u=PACK))
-        q_raw = [q_first[:]]
-        for c in range(1, CHUNKS):
-            q_late = reused.tile([P, PACK, W], F32, name=f"q_late{c}", offset=c * PACK * W * 4)
-            nc.sync.dma_start(q_late[:], q_rows[:, :, cols[c]])
-            q_raw.append(q_late[:])
 
         scale_listed = sb.tile([P, N], U8, name="scale_listed")
         nc.vector.tensor_copy(scale_listed[:], scale_pool[:].indirect(offsets[:]))
@@ -91,45 +92,42 @@ def tile_attend_plw_decay_srt_kernel(tc, qT, k_words, k_scales, dk, dc, offs, ou
             scale_listed[:].rearrange("p (m t) -> p t m", t=PACK),
         )
 
-        dc_bank = ps.tile([P, PACK, P], F32, name="dc_bank", tag="dc_then_last")
+        dc_bank = ps.tile([P, PACK, P], F32, name="dc_bank", tag="bank_dc")
         for u in range(PACK):
             nc.tensor.transpose(dc_bank[:, u, :], dc_quads[:, u : u + 1].to_broadcast([P, P]), ident[:])
         dc_rows = sb.tile([P, NQ], F32, name="dc_rows")
         nc.scalar.copy(dc_rows[:].rearrange("p (n u) -> p n u", u=PACK), dc_bank[:].rearrange("p u n -> p n u"))
 
-        dk_bank = ps.tile([P, PACK, P], F32, name="dk_bank")
+        dk_bank = ps.tile([P, PACK, P], F32, name="dk_bank", tag="bank_dk")
         dk_dealt = dk_listed[:].rearrange("p (m t) -> p t m", t=PACK)
         for t in range(PACK):
             nc.tensor.transpose(dk_bank[:, t, :], dk_dealt[:, t, :], ident[:])
+        dk_slots = sb.tile([P, PACK], F32, name="dk_slots")
+        nc.scalar.copy(dk_slots[:], dk_bank[:, :, P - 1])
 
-        q_codes, q_scale = [], []
-        for c in range(CHUNKS):
-            q_woven = sb.tile([P, W, PACK], BF16, name=f"q_woven{c}", align_bytes=64)
-            weave(nc.scalar.copy, q_woven[:], q_raw[c])
-            q_codes.append(sb.tile([P, W], U32, name=f"q_codes{c}", align_bytes=64))
-            q_scale.append(sb.tile([P, W], U8, name=f"q_scale{c}", align_bytes=64))
-            nc.vector.quantize_mx(
-                out=q_codes[c][:].bitcast(FP8X4),
-                scales=q_scale[c][:],
-                in_=q_woven[:].rearrange("p w t -> p (w t)"),
-            )
+        q_scale = [sb.tile([P, W], U8, name=f"q_scale{c}", align_bytes=64) for c in range(CHUNKS)]
+        q_codes = [reused.tile([P, W], U32, name="q_codes0", offset=0, align_bytes=64)]
+        q_left = sb.tile([P, HALF, PACK], BF16, name="q_left", align_bytes=64)
+        q_right = reused.tile([P, HALF, PACK], BF16, name="q_right", offset=W * 4, align_bytes=64)
+        weave(nc.scalar.copy, q_left[:], q_raw[0][:, :, 0:HALF])
+        weave(nc.vector.tensor_copy, q_right[:], q_raw[0][:, :, HALF:W])
+        quantize(nc, q_codes[0][:, 0:HALF], q_scale[0][:, 0:HALF], q_left[:])
+        quantize(nc, q_codes[0][:, HALF:W], q_scale[0][:, HALF:W], q_right[:])
+        q_second = sb.tile([P, W, PACK], BF16, name="q_second", align_bytes=64)
+        weave(nc.scalar.copy, q_second[:], q_raw[1][:])
 
         y_rows = out_0.rearrange("(p t) q -> p t q", t=PACK)
         y_words = out_1[0].rearrange("p q u -> p (q u)").bitcast(I32)
         y_codes = sb.tile([P, NQ], U32, name="y_codes", align_bytes=64)
         y_scale = sb.tile([P, NQ], U8, name="y_scale", align_bytes=64)
-        ys = []
+        ys = [sb.tile([P, PACK, W], F32, name=f"y{c}") for c in range(CHUNKS)]
+        y_woven = [sb.tile([P, W, PACK], BF16, name=f"y_woven{c}", align_bytes=64) for c in range(CHUNKS)]
+        bank_tags = [["bank_0", "bank_1", "bank_2", "bank_3"], ["bank_4", "bank_5", "bank_dc", "bank_dk"]]
         for c in range(CHUNKS):
-            if c == 0:
-                scores = [ps.tile([P, W], F32, name=f"score0_{t}")[:] for t in range(PACK)]
-            else:
-                bank = ps.tile([P, PACK, W], F32, name=f"score{c}", tag="dc_then_last" if c == CHUNKS - 1 else f"score{c}")
-                scores = [bank[:, t, :] for t in range(PACK)]
-            y = sb.tile([P, PACK, W], F32, name=f"y{c}")
-            ys.append(y)
+            scores = [ps.tile([P, W], F32, name=f"score{c}_{t}", tag=bank_tags[c][t]) for t in range(PACK)]
             for t in range(PACK):
                 nc.tensor.matmul_mx(
-                    out=scores[t],
+                    out=scores[t][:],
                     lhsT=k_codes[:, t * P : (t + 1) * P].bitcast(FP8X4),
                     lhsT_scale=k_scale[:, t * P : (t + 1) * P],
                     rhs=q_codes[c][:].bitcast(FP8X4),
@@ -139,27 +137,28 @@ def tile_attend_plw_decay_srt_kernel(tc, qT, k_words, k_scales, dk, dc, offs, ou
                 )
             for t in range(PACK):
                 nc.vector.scalar_tensor_tensor(
-                    out=y[:, t, :],
-                    in0=scores[t],
-                    scalar=dk_bank[:, t, P - 1 : P],
+                    out=ys[c][:, t, :],
+                    in0=scores[t][:],
+                    scalar=dk_slots[:, t : t + 1],
                     in1=dc_rows[:, cols[c]],
                     op0=MULT,
                     op1=MULT,
                 )
-            nc.sync.dma_start(y_rows[:, :, cols[c]], y[:])
-            y_woven = sb.tile([P, W, PACK], BF16, name=f"y_woven{c}", align_bytes=64)
-            weave(nc.vector.tensor_copy if c == CHUNKS - 1 else nc.scalar.copy, y_woven[:], y[:])
-            nc.vector.quantize_mx(
-                out=y_codes[:, cols[c]].bitcast(FP8X4),
-                scales=y_scale[:, cols[c]],
-                in_=y_woven[:].rearrange("p w t -> p (w t)"),
-            )
-            if c > 0:
-                done = slice(0, 2 * W) if c == 1 else cols[c]
-                queue = nc.scalar if c == CHUNKS - 1 else nc.sync
-                queue.dma_start(y_words[:, done], y_codes[:, done].bitcast(I32))
+                if c == 0 and t == 1:
+                    q_codes.append(reused.tile([P, W], U32, name="q_codes1", offset=0, align_bytes=64))
+                    quantize(nc, q_codes[1][:], q_scale[1][:], q_second[:])
+                if t % 2 == 1:
+                    nc.sync.dma_start(y_rows[:, t - 1 : t + 1, cols[c]], ys[c][:, t - 1 : t + 1, :])
+            if c == 0:
+                weave(nc.scalar.copy, y_woven[0][:], ys[0][:])
+        quantize(nc, y_codes[:, cols[0]], y_scale[:, cols[0]], y_woven[0][:])
+        nc.sync.dma_start(y_words[:, cols[0]], y_codes[:, cols[0]].bitcast(I32))
+        weave(nc.scalar.copy, y_woven[1][:, 0:HALF, :], ys[1][:, :, 0:HALF])
+        weave(nc.vector.tensor_copy, y_woven[1][:, HALF:W, :], ys[1][:, :, HALF:W])
+        quantize(nc, y_codes[:, cols[1]], y_scale[:, cols[1]], y_woven[1][:])
+        nc.sync.dma_start(y_words[:, cols[1]], y_codes[:, cols[1]].bitcast(I32))
         for quad in range(4):
-            queue = nc.scalar if quad == 0 else nc.sync
+            queue = nc.scalar if quad % 2 == 0 else nc.sync
             queue.dma_start(
                 out_2[0, 4 * quad : 4 * quad + 4, :].bitcast(I32),
                 y_scale[32 * quad : 32 * quad + 4, :].bitcast(I32),

@@ -21,7 +21,8 @@ NQ = 512
 W = 256
 HALF = W // 2
 CHUNKS = NQ // W
-SPLIT = 1152
+SPLIT = 1088
+TAIL = 160
 
 FLOPS = 2 * N * D * NQ
 BYTES = 4 * D * NQ + D * T + 16 * T + 4 * T + 4 * NQ + 2 * P * N // 16 + 4 * N * NQ + N * NQ + 16 * NQ
@@ -43,20 +44,22 @@ def tile_attend_plw_decay_srt_kernel(tc, qT, k_words, k_scales, dk, dc, offs, ou
     cols = [slice(c * W, (c + 1) * W) for c in range(CHUNKS)]
     with ExitStack() as ctx:
         sb = ctx.enter_context(tc.tile_pool(name="sb", bufs=1))
-        reused = ctx.enter_context(tc.tile_pool(name="reused", bufs=1))
+        shared = ctx.enter_context(tc.tile_pool(name="shared", bufs=1))
         ps = ctx.enter_context(tc.psum_pool(name="ps", bufs=1))
+
+        def placed(shape, dtype, name, offset):
+            return shared.tile(shape, dtype, name=name, offset=offset, align_bytes=64)
 
         offsets = sb.tile([P, N // 16], U16, name="offsets")
         dk_pool = sb.tile([P, T], F32, name="dk_pool")
-        word_pool = reused.tile([P, T], U32, name="word_pool", offset=0, align_bytes=64)
+        word_pool = sb.tile([P, T], U32, name="word_pool")
         scale_pool = sb.tile([P, T], U8, name="scale_pool")
-        ident = sb.tile([P, P], F32, name="ident")
+        ident = placed([P, P], F32, "ident", 6144)
         dc_quads = sb.tile([P, PACK], F32, name="dc_quads")
-        q_raw = [sb.tile([P, PACK, W], F32, name=f"q_raw{c}") for c in range(CHUNKS)]
+        q_raw = [placed([P, PACK, W], F32, "q_raw0", 0), sb.tile([P, PACK, W], F32, name="q_raw1")]
 
         scale_zero = scale_pool[:].bitcast(I32)
-        nc.vector.memset(scale_zero[:, 0 : T // 8], 0)
-        nc.gpsimd.memset(scale_zero[:, T // 8 : T // 4], 0)
+        nc.gpsimd.memset(scale_zero, 0)
         dk_zero = dk_pool[0 : P - 1, :].bitcast(I32)
         nc.vector.memset(dk_zero[:, 0 : SPLIT - 1], 0)
         nc.vector.memset(dk_zero[:, SPLIT - 1 : SPLIT], 0)
@@ -66,7 +69,7 @@ def tile_attend_plw_decay_srt_kernel(tc, qT, k_words, k_scales, dk, dc, offs, ou
         q_rows = qT[0].rearrange("(p t) q -> p t q", t=PACK)
         nc.sync.dma_start(offsets[:], offs)
         nc.sync.dma_start(dk_pool[P - 1 : P, :], dk[0:1, :])
-        nc.sync.dma_start(dc_quads[:], dc[0, 0].rearrange("(p u) -> p u", u=PACK))
+        nc.sync.dma_start(q_raw[0][:], q_rows[:, :, cols[0]])
         for quad in range(4):
             queue = nc.scalar if quad < 2 else nc.sync
             queue.dma_start(
@@ -74,23 +77,36 @@ def tile_attend_plw_decay_srt_kernel(tc, qT, k_words, k_scales, dk, dc, offs, ou
                 k_scales[0, 4 * quad : 4 * quad + 4, :].bitcast(I32),
             )
         nc.sync.dma_start(word_pool[:].bitcast(I32), k_words[0].rearrange("p n r -> p (n r)").bitcast(I32))
-        for c in range(CHUNKS):
-            nc.sync.dma_start(q_raw[c][:], q_rows[:, :, cols[c]])
+        nc.sync.dma_start(dc_quads[:], dc[0, 0].rearrange("(p u) -> p u", u=PACK))
+        nc.sync.dma_start(q_raw[1][:], q_rows[:, :, cols[1]])
 
         dk_listed = sb.tile([P, N], F32, name="dk_listed")
         nc.vector.tensor_copy(dk_listed[:], dk_pool[:].indirect(offsets[:]))
-
         scale_listed = sb.tile([P, N], U8, name="scale_listed")
         nc.vector.tensor_copy(scale_listed[:], scale_pool[:].indirect(offsets[:]))
-        k_codes = sb.tile([P, N], U32, name="k_codes", align_bytes=64)
-        nc.vector.tensor_copy(
-            k_codes[:].rearrange("p (t m) -> p m t", t=PACK), word_pool[:].indirect(offsets[:])
-        )
-        k_scale = sb.tile([P, N], U8, name="k_scale", align_bytes=64)
+
+        q_woven = [placed([P, W, PACK], BF16, "q_woven0", 4096)]
+        q_codes = [placed([P, W], U32, "q_codes0", 8192)]
+        q_scale = [sb.tile([P, W], U8, name=f"q_scale{c}", align_bytes=64) for c in range(CHUNKS)]
+        weave(nc.scalar.copy, q_woven[0][:], q_raw[0][:])
+        quantize(nc, q_codes[0][:], q_scale[0][:], q_woven[0][:])
+
+        k_scale = placed([P, N], U8, "k_scale", 0)
         nc.vector.tensor_copy(
             k_scale[:].rearrange("p (t m) -> p t m", t=PACK),
             scale_listed[:].rearrange("p (m t) -> p t m", t=PACK),
         )
+        k_codes = placed([P, N], U32, "k_codes", 4096)
+        nc.vector.tensor_copy(
+            k_codes[:].rearrange("p (t m) -> p m t", t=PACK), word_pool[:].indirect(offsets[:])
+        )
+
+        dk_bank = ps.tile([P, PACK, P], F32, name="dk_bank", tag="bank_dk")
+        dk_dealt = dk_listed[:].rearrange("p (m t) -> p t m", t=PACK)
+        for t in range(PACK):
+            nc.tensor.transpose(dk_bank[:, t, :], dk_dealt[:, t, :], ident[:])
+        dk_slots = placed([P, PACK], F32, "dk_slots", 512)
+        nc.scalar.copy(dk_slots[:], dk_bank[:, :, P - 1])
 
         dc_bank = ps.tile([P, PACK, P], F32, name="dc_bank", tag="bank_dc")
         for u in range(PACK):
@@ -98,31 +114,14 @@ def tile_attend_plw_decay_srt_kernel(tc, qT, k_words, k_scales, dk, dc, offs, ou
         dc_rows = sb.tile([P, NQ], F32, name="dc_rows")
         nc.scalar.copy(dc_rows[:].rearrange("p (n u) -> p n u", u=PACK), dc_bank[:].rearrange("p u n -> p n u"))
 
-        dk_bank = ps.tile([P, PACK, P], F32, name="dk_bank", tag="bank_dk")
-        dk_dealt = dk_listed[:].rearrange("p (m t) -> p t m", t=PACK)
-        for t in range(PACK):
-            nc.tensor.transpose(dk_bank[:, t, :], dk_dealt[:, t, :], ident[:])
-        dk_slots = sb.tile([P, PACK], F32, name="dk_slots")
-        nc.scalar.copy(dk_slots[:], dk_bank[:, :, P - 1])
-
-        q_scale = [sb.tile([P, W], U8, name=f"q_scale{c}", align_bytes=64) for c in range(CHUNKS)]
-        q_codes = [reused.tile([P, W], U32, name="q_codes0", offset=0, align_bytes=64)]
-        q_left = sb.tile([P, HALF, PACK], BF16, name="q_left", align_bytes=64)
-        q_right = reused.tile([P, HALF, PACK], BF16, name="q_right", offset=W * 4, align_bytes=64)
-        weave(nc.scalar.copy, q_left[:], q_raw[0][:, :, 0:HALF])
-        weave(nc.vector.tensor_copy, q_right[:], q_raw[0][:, :, HALF:W])
-        quantize(nc, q_codes[0][:, 0:HALF], q_scale[0][:, 0:HALF], q_left[:])
-        quantize(nc, q_codes[0][:, HALF:W], q_scale[0][:, HALF:W], q_right[:])
-        q_second = sb.tile([P, W, PACK], BF16, name="q_second", align_bytes=64)
-        weave(nc.scalar.copy, q_second[:], q_raw[1][:])
+        q_woven.append(placed([P, W, PACK], BF16, "q_woven1", 6144))
+        weave(nc.scalar.copy, q_woven[1][:], q_raw[1][:])
 
         y_rows = out_0.rearrange("(p t) q -> p t q", t=PACK)
         y_words = out_1[0].rearrange("p q u -> p (q u)").bitcast(I32)
-        y_codes = sb.tile([P, NQ], U32, name="y_codes", align_bytes=64)
-        y_scale = sb.tile([P, NQ], U8, name="y_scale", align_bytes=64)
         ys = [sb.tile([P, PACK, W], F32, name=f"y{c}") for c in range(CHUNKS)]
         y_woven = [sb.tile([P, W, PACK], BF16, name=f"y_woven{c}", align_bytes=64) for c in range(CHUNKS)]
-        bank_tags = [["bank_0", "bank_1", "bank_2", "bank_3"], ["bank_4", "bank_5", "bank_dc", "bank_dk"]]
+        bank_tags = [["bank_0", "bank_1", "bank_2", "bank_3"], ["bank_4", "bank_5", "bank_dk", "bank_dc"]]
         for c in range(CHUNKS):
             scores = [ps.tile([P, W], F32, name=f"score{c}_{t}", tag=bank_tags[c][t]) for t in range(PACK)]
             for t in range(PACK):
@@ -145,16 +144,18 @@ def tile_attend_plw_decay_srt_kernel(tc, qT, k_words, k_scales, dk, dc, offs, ou
                     op1=MULT,
                 )
                 if c == 0 and t == 1:
-                    q_codes.append(reused.tile([P, W], U32, name="q_codes1", offset=0, align_bytes=64))
-                    quantize(nc, q_codes[1][:], q_scale[1][:], q_second[:])
+                    q_codes.append(placed([P, W], U32, "q_codes1", 8192))
+                    quantize(nc, q_codes[1][:], q_scale[1][:], q_woven[1][:])
                 if t % 2 == 1:
                     nc.sync.dma_start(y_rows[:, t - 1 : t + 1, cols[c]], ys[c][:, t - 1 : t + 1, :])
             if c == 0:
                 weave(nc.scalar.copy, y_woven[0][:], ys[0][:])
+        y_codes = placed([P, NQ], U32, "y_codes", 8192)
+        y_scale = sb.tile([P, NQ], U8, name="y_scale", align_bytes=64)
         quantize(nc, y_codes[:, cols[0]], y_scale[:, cols[0]], y_woven[0][:])
         nc.sync.dma_start(y_words[:, cols[0]], y_codes[:, cols[0]].bitcast(I32))
-        weave(nc.scalar.copy, y_woven[1][:, 0:HALF, :], ys[1][:, :, 0:HALF])
-        weave(nc.vector.tensor_copy, y_woven[1][:, HALF:W, :], ys[1][:, :, HALF:W])
+        weave(nc.scalar.copy, y_woven[1][:, 0:TAIL, :], ys[1][:, :, 0:TAIL])
+        weave(nc.vector.tensor_copy, y_woven[1][:, TAIL:W, :], ys[1][:, :, TAIL:W])
         quantize(nc, y_codes[:, cols[1]], y_scale[:, cols[1]], y_woven[1][:])
         nc.sync.dma_start(y_words[:, cols[1]], y_codes[:, cols[1]].bitcast(I32))
         for quad in range(4):

@@ -11,6 +11,7 @@ U16 = mybir.dt.uint16
 U8 = mybir.dt.uint8
 FP8X4 = mybir.dt.float8_e4m3fn_x4
 MULT = mybir.AluOpType.mult
+COPY = mybir.ActivationFunctionType.Copy
 
 P = 128
 PACK = 4
@@ -22,7 +23,9 @@ W = 256
 HALF = W // 2
 CHUNKS = NQ // W
 SPLIT = 1088
-TAIL = 160
+TAIL = 80
+SHARED_PLACE = (0, 0)
+REACH = T - N // 2
 
 FLOPS = 2 * N * D * NQ
 BYTES = 4 * D * NQ + D * T + 16 * T + 4 * T + 4 * NQ + 2 * P * N // 16 + 4 * N * NQ + N * NQ + 16 * NQ
@@ -52,11 +55,11 @@ def tile_attend_plw_decay_srt_kernel(tc, qT, k_words, k_scales, dk, dc, offs, ou
 
         offsets = sb.tile([P, N // 16], U16, name="offsets")
         dk_pool = sb.tile([P, T], F32, name="dk_pool")
-        word_pool = sb.tile([P, T], U32, name="word_pool")
+        word_pool = placed([P, T], U32, "word_pool", 10240)
         scale_pool = sb.tile([P, T], U8, name="scale_pool")
         ident = placed([P, P], F32, "ident", 6144)
         dc_quads = sb.tile([P, PACK], F32, name="dc_quads")
-        q_raw = [placed([P, PACK, W], F32, "q_raw0", 0), sb.tile([P, PACK, W], F32, name="q_raw1")]
+        q_raw = [placed([P, PACK, W], F32, "q_raw0", 0), placed([P, PACK, W], F32, "q_raw1", 18432)]
 
         scale_zero = scale_pool[:].bitcast(I32)
         nc.gpsimd.memset(scale_zero, 0)
@@ -76,8 +79,10 @@ def tile_attend_plw_decay_srt_kernel(tc, qT, k_words, k_scales, dk, dc, offs, ou
                 scale_pool[32 * quad : 32 * quad + 4, :].bitcast(I32),
                 k_scales[0, 4 * quad : 4 * quad + 4, :].bitcast(I32),
             )
-        nc.sync.dma_start(word_pool[:].bitcast(I32), k_words[0].rearrange("p n r -> p (n r)").bitcast(I32))
+        word_rows = k_words[0].rearrange("p n r -> p (n r)").bitcast(I32)
+        nc.sync.dma_start(word_pool[:, 0:REACH].bitcast(I32), word_rows[:, 0:REACH])
         nc.sync.dma_start(dc_quads[:], dc[0, 0].rearrange("(p u) -> p u", u=PACK))
+        nc.sync.dma_start(word_pool[:, REACH:T].bitcast(I32), word_rows[:, REACH:T])
         nc.sync.dma_start(q_raw[1][:], q_rows[:, :, cols[1]])
 
         dk_listed = sb.tile([P, N], F32, name="dk_listed")
@@ -97,9 +102,9 @@ def tile_attend_plw_decay_srt_kernel(tc, qT, k_words, k_scales, dk, dc, offs, ou
             scale_listed[:].rearrange("p (m t) -> p t m", t=PACK),
         )
         k_codes = placed([P, N], U32, "k_codes", 4096)
-        nc.vector.tensor_copy(
-            k_codes[:].rearrange("p (t m) -> p m t", t=PACK), word_pool[:].indirect(offsets[:])
-        )
+        codes_dealt = k_codes[:].rearrange("p (t m) -> p m t", t=PACK)
+        nc.vector.tensor_copy(codes_dealt[:, 0 : P // 2, :], word_pool[:, 0:REACH].indirect(offsets[:, 0 : N // 32]))
+        nc.vector.tensor_copy(codes_dealt[:, P // 2 : P, :], word_pool[:].indirect(offsets[:, N // 32 : N // 16]))
 
         dk_bank = ps.tile([P, PACK, P], F32, name="dk_bank", tag="bank_dk")
         dk_dealt = dk_listed[:].rearrange("p (m t) -> p t m", t=PACK)
@@ -107,20 +112,25 @@ def tile_attend_plw_decay_srt_kernel(tc, qT, k_words, k_scales, dk, dc, offs, ou
             nc.tensor.transpose(dk_bank[:, t, :], dk_dealt[:, t, :], ident[:])
         dk_slots = placed([P, PACK], F32, "dk_slots", 512)
         nc.scalar.copy(dk_slots[:], dk_bank[:, :, P - 1])
+        dk_own = placed([P, PACK], F32, "dk_own", 2048)
+        nc.scalar.copy(dk_own[:], dk_bank[:, :, P - 1])
 
         dc_bank = ps.tile([P, PACK, P], F32, name="dc_bank", tag="bank_dc")
         for u in range(PACK):
             nc.tensor.transpose(dc_bank[:, u, :], dc_quads[:, u : u + 1].to_broadcast([P, P]), ident[:])
-        dc_rows = sb.tile([P, NQ], F32, name="dc_rows")
+        dc_rows = placed([P, NQ], F32, "dc_rows", 22528)
         nc.scalar.copy(dc_rows[:].rearrange("p (n u) -> p n u", u=PACK), dc_bank[:].rearrange("p u n -> p n u"))
 
-        q_woven.append(placed([P, W, PACK], BF16, "q_woven1", 6144))
-        weave(nc.scalar.copy, q_woven[1][:], q_raw[1][:])
+        q_woven.append(placed([P, W, PACK], BF16, "q_woven1", 10240))
+        weave(nc.scalar.copy, q_woven[1][:, 0:HALF, :], q_raw[1][:, :, 0:HALF])
+        weave(nc.vector.tensor_copy, q_woven[1][:, HALF:W, :], q_raw[1][:, :, HALF:W])
+        q_codes.append(placed([P, W], U32, "q_codes1", 9216))
+        quantize(nc, q_codes[1][:], q_scale[1][:], q_woven[1][:])
 
         y_rows = out_0.rearrange("(p t) q -> p t q", t=PACK)
         y_words = out_1[0].rearrange("p q u -> p (q u)").bitcast(I32)
-        ys = [sb.tile([P, PACK, W], F32, name=f"y{c}") for c in range(CHUNKS)]
-        y_woven = [sb.tile([P, W, PACK], BF16, name=f"y_woven{c}", align_bytes=64) for c in range(CHUNKS)]
+        ys = [placed([P, PACK, W], F32, "y0", 10240), sb.tile([P, PACK, W], F32, name="y1")]
+        y_woven = [placed([P, W, PACK], BF16, "y_woven0", 2048), sb.tile([P, W, PACK], BF16, name="y_woven1", align_bytes=64)]
         bank_tags = [["bank_0", "bank_1", "bank_2", "bank_3"], ["bank_4", "bank_5", "bank_dk", "bank_dc"]]
         for c in range(CHUNKS):
             scores = [ps.tile([P, W], F32, name=f"score{c}_{t}", tag=bank_tags[c][t]) for t in range(PACK)]
@@ -135,27 +145,29 @@ def tile_attend_plw_decay_srt_kernel(tc, qT, k_words, k_scales, dk, dc, offs, ou
                     stop=True,
                 )
             for t in range(PACK):
-                nc.vector.scalar_tensor_tensor(
-                    out=ys[c][:, t, :],
-                    in0=scores[t][:],
-                    scalar=dk_slots[:, t : t + 1],
-                    in1=dc_rows[:, cols[c]],
-                    op0=MULT,
-                    op1=MULT,
-                )
-                if c == 0 and t == 1:
-                    q_codes.append(placed([P, W], U32, "q_codes1", 8192))
-                    quantize(nc, q_codes[1][:], q_scale[1][:], q_woven[1][:])
+                if t == SHARED_PLACE[c]:
+                    scaled = placed([P, W], F32, f"scaled{c}", 18432 + 4 * W * c)
+                    nc.scalar.activation(scaled[:], scores[t][:], COPY, scale=dk_own[:, t : t + 1])
+                    nc.gpsimd.tensor_tensor(ys[c][:, t, :], scaled[:], dc_rows[:, cols[c]], MULT)
+                    if c == 1:
+                        weave(nc.scalar.copy, y_woven[0][:], ys[0][:])
+                else:
+                    nc.vector.scalar_tensor_tensor(
+                        out=ys[c][:, t, :],
+                        in0=scores[t][:],
+                        scalar=dk_slots[:, t : t + 1],
+                        in1=dc_rows[:, cols[c]],
+                        op0=MULT,
+                        op1=MULT,
+                    )
                 if t % 2 == 1:
                     nc.sync.dma_start(y_rows[:, t - 1 : t + 1, cols[c]], ys[c][:, t - 1 : t + 1, :])
-            if c == 0:
-                weave(nc.scalar.copy, y_woven[0][:], ys[0][:])
-        y_codes = placed([P, NQ], U32, "y_codes", 8192)
+        y_codes = placed([P, NQ], U32, "y_codes", 22528)
         y_scale = sb.tile([P, NQ], U8, name="y_scale", align_bytes=64)
-        quantize(nc, y_codes[:, cols[0]], y_scale[:, cols[0]], y_woven[0][:])
-        nc.sync.dma_start(y_words[:, cols[0]], y_codes[:, cols[0]].bitcast(I32))
         weave(nc.scalar.copy, y_woven[1][:, 0:TAIL, :], ys[1][:, :, 0:TAIL])
         weave(nc.vector.tensor_copy, y_woven[1][:, TAIL:W, :], ys[1][:, :, TAIL:W])
+        quantize(nc, y_codes[:, cols[0]], y_scale[:, cols[0]], y_woven[0][:])
+        nc.sync.dma_start(y_words[:, cols[0]], y_codes[:, cols[0]].bitcast(I32))
         quantize(nc, y_codes[:, cols[1]], y_scale[:, cols[1]], y_woven[1][:])
         nc.sync.dma_start(y_words[:, cols[1]], y_codes[:, cols[1]].bitcast(I32))
         for quad in range(4):

@@ -24,6 +24,7 @@ HALF = W // 2
 CHUNKS = NQ // W
 SPLIT = 1088
 TAIL = 80
+LEFT = 96
 SHARED_PLACE = (0, 0)
 REACH = T - N // 2
 
@@ -118,18 +119,18 @@ def tile_attend_plw_decay_srt_kernel(tc, qT, k_words, k_scales, dk, dc, offs, ou
         dc_bank = ps.tile([P, PACK, P], F32, name="dc_bank", tag="bank_dc")
         for u in range(PACK):
             nc.tensor.transpose(dc_bank[:, u, :], dc_quads[:, u : u + 1].to_broadcast([P, P]), ident[:])
-        dc_rows = placed([P, NQ], F32, "dc_rows", 22528)
+        dc_rows = placed([P, NQ], F32, "dc_rows", 24576)
         nc.scalar.copy(dc_rows[:].rearrange("p (n u) -> p n u", u=PACK), dc_bank[:].rearrange("p u n -> p n u"))
 
         q_woven.append(placed([P, W, PACK], BF16, "q_woven1", 10240))
-        weave(nc.scalar.copy, q_woven[1][:, 0:HALF, :], q_raw[1][:, :, 0:HALF])
-        weave(nc.vector.tensor_copy, q_woven[1][:, HALF:W, :], q_raw[1][:, :, HALF:W])
+        weave(nc.scalar.copy, q_woven[1][:, 0:LEFT, :], q_raw[1][:, :, 0:LEFT])
+        weave(nc.vector.tensor_copy, q_woven[1][:, LEFT:W, :], q_raw[1][:, :, LEFT:W])
         q_codes.append(placed([P, W], U32, "q_codes1", 9216))
         quantize(nc, q_codes[1][:], q_scale[1][:], q_woven[1][:])
 
         y_rows = out_0.rearrange("(p t) q -> p t q", t=PACK)
         y_words = out_1[0].rearrange("p q u -> p (q u)").bitcast(I32)
-        ys = [placed([P, PACK, W], F32, "y0", 10240), sb.tile([P, PACK, W], F32, name="y1")]
+        ys = [placed([P, PACK, W], F32, "y0", 20480), sb.tile([P, PACK, W], F32, name="y1")]
         y_woven = [placed([P, W, PACK], BF16, "y_woven0", 2048), sb.tile([P, W, PACK], BF16, name="y_woven1", align_bytes=64)]
         bank_tags = [["bank_0", "bank_1", "bank_2", "bank_3"], ["bank_4", "bank_5", "bank_dk", "bank_dc"]]
         for c in range(CHUNKS):
@@ -160,9 +161,12 @@ def tile_attend_plw_decay_srt_kernel(tc, qT, k_words, k_scales, dk, dc, offs, ou
                         op0=MULT,
                         op1=MULT,
                     )
-                if t % 2 == 1:
+                if c == 1 and t % 2 == 1:
                     nc.sync.dma_start(y_rows[:, t - 1 : t + 1, cols[c]], ys[c][:, t - 1 : t + 1, :])
-        y_codes = placed([P, NQ], U32, "y_codes", 22528)
+            if c == 0:
+                for t in (1, 2, 0, 3):
+                    nc.sync.dma_start(y_rows[:, t, cols[c]], ys[c][:, t, :])
+        y_codes = placed([P, NQ], U32, "y_codes", 24576)
         y_scale = sb.tile([P, NQ], U8, name="y_scale", align_bytes=64)
         weave(nc.scalar.copy, y_woven[1][:, 0:TAIL, :], ys[1][:, :, 0:TAIL])
         weave(nc.vector.tensor_copy, y_woven[1][:, TAIL:W, :], ys[1][:, :, TAIL:W])

@@ -151,7 +151,8 @@ def tile_attend_plw_decay_srt_kernel(tc, qT, k_words, k_scales, dk, dc, offs, ou
                     nc.scalar.activation(scaled[:], scores[t][:], COPY, scale=dk_own[:, t : t + 1])
                     nc.gpsimd.tensor_tensor(ys[c][:, t, :], scaled[:], dc_rows[:, cols[c]], MULT)
                     if c == 1:
-                        weave(nc.scalar.copy, y_woven[0][:], ys[0][:])
+                        weave(nc.scalar.copy, y_woven[0][:, 0:HALF, :], ys[0][:, :, 0:HALF])
+                        weave(nc.scalar.copy, y_woven[0][:, HALF:W, :], ys[0][:, :, HALF:W])
                 else:
                     nc.vector.scalar_tensor_tensor(
                         out=ys[c][:, t, :],
@@ -166,11 +167,12 @@ def tile_attend_plw_decay_srt_kernel(tc, qT, k_words, k_scales, dk, dc, offs, ou
             if c == 0:
                 for t in (1, 2, 0, 3):
                     nc.sync.dma_start(y_rows[:, t, cols[c]], ys[c][:, t, :])
-        y_codes = placed([P, NQ], U32, "y_codes", 24576)
+        y_codes = placed([P, NQ], U32, "y_codes", 8192)
         y_scale = sb.tile([P, NQ], U8, name="y_scale", align_bytes=64)
+        quantize(nc, y_codes[:, 0:HALF], y_scale[:, 0:HALF], y_woven[0][:, 0:HALF, :])
         weave(nc.scalar.copy, y_woven[1][:, 0:TAIL, :], ys[1][:, :, 0:TAIL])
         weave(nc.vector.tensor_copy, y_woven[1][:, TAIL:W, :], ys[1][:, :, TAIL:W])
-        quantize(nc, y_codes[:, cols[0]], y_scale[:, cols[0]], y_woven[0][:])
+        quantize(nc, y_codes[:, HALF:W], y_scale[:, HALF:W], y_woven[0][:, HALF:W, :])
         nc.sync.dma_start(y_words[:, cols[0]], y_codes[:, cols[0]].bitcast(I32))
         quantize(nc, y_codes[:, cols[1]], y_scale[:, cols[1]], y_woven[1][:])
         nc.sync.dma_start(y_words[:, cols[1]], y_codes[:, cols[1]].bitcast(I32))

@@ -23,9 +23,12 @@ W = 256
 HALF = W // 2
 CHUNKS = NQ // W
 SPLIT = 1088
-TAIL = 80
+TAIL = 112
+STORES = (
+    (slice(1, 2), slice(2, 3), slice(0, 1), slice(3, 4)),
+    (slice(0, 2), slice(2, 4)),
+)
 LEFT = 96
-SHARED_PLACE = (0, 0)
 REACH = T - N // 2
 
 FLOPS = 2 * N * D * NQ
@@ -113,8 +116,6 @@ def tile_attend_plw_decay_srt_kernel(tc, qT, k_words, k_scales, dk, dc, offs, ou
             nc.tensor.transpose(dk_bank[:, t, :], dk_dealt[:, t, :], ident[:])
         dk_slots = placed([P, PACK], F32, "dk_slots", 512)
         nc.scalar.copy(dk_slots[:], dk_bank[:, :, P - 1])
-        dk_own = placed([P, PACK], F32, "dk_own", 2048)
-        nc.scalar.copy(dk_own[:], dk_bank[:, :, P - 1])
 
         dc_bank = ps.tile([P, PACK, P], F32, name="dc_bank", tag="bank_dc")
         for u in range(PACK):
@@ -131,7 +132,7 @@ def tile_attend_plw_decay_srt_kernel(tc, qT, k_words, k_scales, dk, dc, offs, ou
         y_rows = out_0.rearrange("(p t) q -> p t q", t=PACK)
         y_words = out_1[0].rearrange("p q u -> p (q u)").bitcast(I32)
         ys = [placed([P, PACK, W], F32, "y0", 20480), sb.tile([P, PACK, W], F32, name="y1")]
-        y_woven = [placed([P, W, PACK], BF16, "y_woven0", 2048), sb.tile([P, W, PACK], BF16, name="y_woven1", align_bytes=64)]
+        y_woven = [sb.tile([P, W, PACK], BF16, name="y_woven0", align_bytes=64), sb.tile([P, W, PACK], BF16, name="y_woven1", align_bytes=64)]
         bank_tags = [["bank_0", "bank_1", "bank_2", "bank_3"], ["bank_4", "bank_5", "bank_dk", "bank_dc"]]
         for c in range(CHUNKS):
             scores = [ps.tile([P, W], F32, name=f"score{c}_{t}", tag=bank_tags[c][t]) for t in range(PACK)]
@@ -146,13 +147,10 @@ def tile_attend_plw_decay_srt_kernel(tc, qT, k_words, k_scales, dk, dc, offs, ou
                     stop=True,
                 )
             for t in range(PACK):
-                if t == SHARED_PLACE[c]:
+                if c == 0 and t == 0:
                     scaled = placed([P, W], F32, f"scaled{c}", 18432 + 4 * W * c)
-                    nc.scalar.activation(scaled[:], scores[t][:], COPY, scale=dk_own[:, t : t + 1])
+                    nc.scalar.activation(scaled[:], scores[t][:], COPY, scale=dk_slots[:, t : t + 1])
                     nc.gpsimd.tensor_tensor(ys[c][:, t, :], scaled[:], dc_rows[:, cols[c]], MULT)
-                    if c == 1:
-                        weave(nc.scalar.copy, y_woven[0][:, 0:HALF, :], ys[0][:, :, 0:HALF])
-                        weave(nc.scalar.copy, y_woven[0][:, HALF:W, :], ys[0][:, :, HALF:W])
                 else:
                     nc.vector.scalar_tensor_tensor(
                         out=ys[c][:, t, :],
@@ -162,11 +160,11 @@ def tile_attend_plw_decay_srt_kernel(tc, qT, k_words, k_scales, dk, dc, offs, ou
                         op0=MULT,
                         op1=MULT,
                     )
-                if c == 1 and t % 2 == 1:
-                    nc.sync.dma_start(y_rows[:, t - 1 : t + 1, cols[c]], ys[c][:, t - 1 : t + 1, :])
             if c == 0:
-                for t in (1, 2, 0, 3):
-                    nc.sync.dma_start(y_rows[:, t, cols[c]], ys[c][:, t, :])
+                weave(nc.scalar.copy, y_woven[0][:, 0:HALF, :], ys[0][:, :, 0:HALF])
+                weave(nc.scalar.copy, y_woven[0][:, HALF:W, :], ys[0][:, :, HALF:W])
+            for places in STORES[c]:
+                nc.sync.dma_start(y_rows[:, places, cols[c]], ys[c][:, places, :])
         y_codes = placed([P, NQ], U32, "y_codes", 8192)
         y_scale = sb.tile([P, NQ], U8, name="y_scale", align_bytes=64)
         quantize(nc, y_codes[:, 0:HALF], y_scale[:, 0:HALF], y_woven[0][:, 0:HALF, :])

@@ -28,7 +28,6 @@ STORES = (
     (slice(1, 2), slice(2, 3), slice(0, 1), slice(3, 4)),
     (slice(0, 2), slice(2, 4)),
 )
-LEFT = 96
 REACH = T - N // 2
 
 FLOPS = 2 * N * D * NQ
@@ -123,11 +122,13 @@ def tile_attend_plw_decay_srt_kernel(tc, qT, k_words, k_scales, dk, dc, offs, ou
         dc_rows = placed([P, NQ], F32, "dc_rows", 24576)
         nc.scalar.copy(dc_rows[:].rearrange("p (n u) -> p n u", u=PACK), dc_bank[:].rearrange("p u n -> p n u"))
 
-        q_woven.append(placed([P, W, PACK], BF16, "q_woven1", 10240))
-        weave(nc.scalar.copy, q_woven[1][:, 0:LEFT, :], q_raw[1][:, :, 0:LEFT])
-        weave(nc.vector.tensor_copy, q_woven[1][:, LEFT:W, :], q_raw[1][:, :, LEFT:W])
+        q_left = placed([P, HALF, PACK], BF16, "q_left", 6144)
+        q_right = placed([P, HALF, PACK], BF16, "q_right", 10240)
+        weave(nc.scalar.copy, q_left[:], q_raw[1][:, :, 0:HALF])
+        weave(nc.vector.tensor_copy, q_right[:], q_raw[1][:, :, HALF:W])
         q_codes.append(placed([P, W], U32, "q_codes1", 9216))
-        quantize(nc, q_codes[1][:], q_scale[1][:], q_woven[1][:])
+        quantize(nc, q_codes[1][:, 0:HALF], q_scale[1][:, 0:HALF], q_left[:])
+        quantize(nc, q_codes[1][:, HALF:W], q_scale[1][:, HALF:W], q_right[:])
 
         y_rows = out_0.rearrange("(p t) q -> p t q", t=PACK)
         y_words = out_1[0].rearrange("p q u -> p (q u)").bitcast(I32)

@@ -59,39 +59,45 @@ def tile_attend_plw_decay_srt_kernel(tc, qT, k_words, k_scales, dk, dc, offs, ou
         offsets = sb.tile([P, N // 16], U16, name="offsets")
         dk_pool = sb.tile([P, T], F32, name="dk_pool")
         word_pool = placed([P, T], U32, "word_pool", 10240)
-        scale_pool = sb.tile([P, T], U8, name="scale_pool")
+        scale_pool = placed([P, T], U8, "scale_pool", 28672)
         ident = placed([P, P], F32, "ident", 6144)
         dc_quads = sb.tile([P, PACK], F32, name="dc_quads")
         q_raw = [placed([P, PACK, W], F32, "q_raw0", 0), placed([P, PACK, W], F32, "q_raw1", 18432)]
 
         scale_zero = scale_pool[:].bitcast(I32)
-        nc.gpsimd.memset(scale_zero, 0)
+        nc.gpsimd.memset(scale_zero[0:48, :], 0)
+        nc.gpsimd.memset(scale_zero[64:P, :], 0)
+        make_identity(nc, ident[:])
         dk_zero = dk_pool[0 : P - 1, :].bitcast(I32)
         nc.vector.memset(dk_zero[:, 0 : SPLIT - 1], 0)
         nc.vector.memset(dk_zero[:, SPLIT - 1 : SPLIT], 0)
         nc.gpsimd.memset(dk_zero[:, SPLIT:T], 0)
-        make_identity(nc, ident[:])
 
         q_rows = qT[0].rearrange("(p t) q -> p t q", t=PACK)
         nc.sync.dma_start(offsets[:], offs)
-        nc.sync.dma_start(dk_pool[P - 1 : P, :], dk[0:1, :])
+        nc.sync.dma_start(scale_pool[48:64, :].bitcast(I32), k_scales[0].bitcast(I32))
         nc.sync.dma_start(q_raw[0][:], q_rows[:, :, cols[0]])
-        for quad in range(4):
-            queue = nc.scalar if quad < 2 else nc.sync
-            queue.dma_start(
-                scale_pool[32 * quad : 32 * quad + 4, :].bitcast(I32),
-                k_scales[0, 4 * quad : 4 * quad + 4, :].bitcast(I32),
-            )
+        nc.sync.dma_start(dk_pool[P - 1 : P, :], dk[0:1, :])
+        nc.sync.dma_start(dc_quads[:], dc[0, 0].rearrange("(p u) -> p u", u=PACK))
         word_rows = k_words[0].rearrange("p n r -> p (n r)").bitcast(I32)
         nc.sync.dma_start(word_pool[:, 0:REACH].bitcast(I32), word_rows[:, 0:REACH])
-        nc.sync.dma_start(dc_quads[:], dc[0, 0].rearrange("(p u) -> p u", u=PACK))
         nc.sync.dma_start(word_pool[:, REACH:T].bitcast(I32), word_rows[:, REACH:T])
         nc.sync.dma_start(q_raw[1][:], q_rows[:, :, cols[1]])
 
-        dk_listed = sb.tile([P, N], F32, name="dk_listed")
-        nc.vector.tensor_copy(dk_listed[:], dk_pool[:].indirect(offsets[:]))
         scale_listed = sb.tile([P, N], U8, name="scale_listed")
         nc.vector.tensor_copy(scale_listed[:], scale_pool[:].indirect(offsets[:]))
+        k_scale = sb.tile([P, N], U8, name="k_scale", align_bytes=64)
+        nc.vector.tensor_copy(
+            k_scale[:].rearrange("p (t m) -> p t m", t=PACK),
+            scale_listed[:].rearrange("p (m t) -> p t m", t=PACK),
+        )
+        for quad in range(4):
+            nc.sync.dma_start(
+                k_scale[32 * quad : 32 * quad + 4, :].bitcast(I32),
+                k_scale[48 + 4 * quad : 52 + 4 * quad, :].bitcast(I32),
+            )
+        dk_listed = placed([P, N], F32, "dk_listed", 28672)
+        nc.vector.tensor_copy(dk_listed[:], dk_pool[:].indirect(offsets[:]))
 
         q_woven = [placed([P, W, PACK], BF16, "q_woven0", 4096)]
         q_codes = [placed([P, W], U32, "q_codes0", 8192)]
@@ -99,15 +105,16 @@ def tile_attend_plw_decay_srt_kernel(tc, qT, k_words, k_scales, dk, dc, offs, ou
         weave(nc.scalar.copy, q_woven[0][:], q_raw[0][:])
         quantize(nc, q_codes[0][:], q_scale[0][:], q_woven[0][:])
 
-        k_scale = placed([P, N], U8, "k_scale", 0)
-        nc.vector.tensor_copy(
-            k_scale[:].rearrange("p (t m) -> p t m", t=PACK),
-            scale_listed[:].rearrange("p (m t) -> p t m", t=PACK),
-        )
         k_codes = placed([P, N], U32, "k_codes", 4096)
         codes_dealt = k_codes[:].rearrange("p (t m) -> p m t", t=PACK)
         nc.vector.tensor_copy(codes_dealt[:, 0 : P // 2, :], word_pool[:, 0:REACH].indirect(offsets[:, 0 : N // 32]))
         nc.vector.tensor_copy(codes_dealt[:, P // 2 : P, :], word_pool[:].indirect(offsets[:, N // 32 : N // 16]))
+
+        dc_bank = ps.tile([P, PACK, P], F32, name="dc_bank", tag="bank_dc")
+        for u in range(PACK):
+            nc.tensor.transpose(dc_bank[:, u, :], dc_quads[:, u : u + 1].to_broadcast([P, P]), ident[:])
+        dc_rows = placed([P, NQ], F32, "dc_rows", 24576)
+        nc.scalar.copy(dc_rows[:].rearrange("p (n u) -> p n u", u=PACK), dc_bank[:].rearrange("p u n -> p n u"))
 
         dk_bank = ps.tile([P, PACK, P], F32, name="dk_bank", tag="bank_dk")
         dk_dealt = dk_listed[:].rearrange("p (m t) -> p t m", t=PACK)
@@ -115,12 +122,6 @@ def tile_attend_plw_decay_srt_kernel(tc, qT, k_words, k_scales, dk, dc, offs, ou
             nc.tensor.transpose(dk_bank[:, t, :], dk_dealt[:, t, :], ident[:])
         dk_slots = placed([P, PACK], F32, "dk_slots", 512)
         nc.scalar.copy(dk_slots[:], dk_bank[:, :, P - 1])
-
-        dc_bank = ps.tile([P, PACK, P], F32, name="dc_bank", tag="bank_dc")
-        for u in range(PACK):
-            nc.tensor.transpose(dc_bank[:, u, :], dc_quads[:, u : u + 1].to_broadcast([P, P]), ident[:])
-        dc_rows = placed([P, NQ], F32, "dc_rows", 24576)
-        nc.scalar.copy(dc_rows[:].rearrange("p (n u) -> p n u", u=PACK), dc_bank[:].rearrange("p u n -> p n u"))
 
         q_left = placed([P, HALF, PACK], BF16, "q_left", 6144)
         q_right = placed([P, HALF, PACK], BF16, "q_right", 10240)

@@ -23,7 +23,6 @@ W = 256
 HALF = W // 2
 CHUNKS = NQ // W
 SPLIT = 1088
-TAIL = 112
 STORES = (
     (slice(1, 2), slice(2, 3), slice(0, 1), slice(3, 4)),
     (slice(0, 2), slice(2, 4)),
@@ -76,8 +75,8 @@ def tile_attend_plw_decay_srt_kernel(tc, qT, k_words, k_scales, dk, dc, offs, ou
         q_rows = qT[0].rearrange("(p t) q -> p t q", t=PACK)
         nc.sync.dma_start(offsets[:], offs)
         nc.sync.dma_start(scale_pool[48:64, :].bitcast(I32), k_scales[0].bitcast(I32))
-        nc.sync.dma_start(q_raw[0][:], q_rows[:, :, cols[0]])
         nc.sync.dma_start(dk_pool[P - 1 : P, :], dk[0:1, :])
+        nc.sync.dma_start(q_raw[0][:], q_rows[:, :, cols[0]])
         nc.sync.dma_start(dc_quads[:], dc[0, 0].rearrange("(p u) -> p u", u=PACK))
         word_rows = k_words[0].rearrange("p n r -> p (n r)").bitcast(I32)
         nc.sync.dma_start(word_pool[:, 0:REACH].bitcast(I32), word_rows[:, 0:REACH])
@@ -105,7 +104,7 @@ def tile_attend_plw_decay_srt_kernel(tc, qT, k_words, k_scales, dk, dc, offs, ou
         weave(nc.scalar.copy, q_woven[0][:], q_raw[0][:])
         quantize(nc, q_codes[0][:], q_scale[0][:], q_woven[0][:])
 
-        k_codes = placed([P, N], U32, "k_codes", 4096)
+        k_codes = sb.tile([P, N], U32, name="k_codes", align_bytes=64)
         codes_dealt = k_codes[:].rearrange("p (t m) -> p m t", t=PACK)
         nc.vector.tensor_copy(codes_dealt[:, 0 : P // 2, :], word_pool[:, 0:REACH].indirect(offsets[:, 0 : N // 32]))
         nc.vector.tensor_copy(codes_dealt[:, P // 2 : P, :], word_pool[:].indirect(offsets[:, N // 32 : N // 16]))
@@ -124,7 +123,7 @@ def tile_attend_plw_decay_srt_kernel(tc, qT, k_words, k_scales, dk, dc, offs, ou
         nc.scalar.copy(dk_slots[:], dk_bank[:, :, P - 1])
 
         q_left = placed([P, HALF, PACK], BF16, "q_left", 6144)
-        q_right = placed([P, HALF, PACK], BF16, "q_right", 10240)
+        q_right = sb.tile([P, HALF, PACK], BF16, name="q_right", align_bytes=64)
         weave(nc.scalar.copy, q_left[:], q_raw[1][:, :, 0:HALF])
         weave(nc.vector.tensor_copy, q_right[:], q_raw[1][:, :, HALF:W])
         q_codes.append(placed([P, W], U32, "q_codes1", 9216))
@@ -169,13 +168,16 @@ def tile_attend_plw_decay_srt_kernel(tc, qT, k_words, k_scales, dk, dc, offs, ou
                 nc.sync.dma_start(y_rows[:, places, cols[c]], ys[c][:, places, :])
         y_codes = placed([P, NQ], U32, "y_codes", 8192)
         y_scale = sb.tile([P, NQ], U8, name="y_scale", align_bytes=64)
+        third = slice(W, W + HALF)
+        fourth = slice(W + HALF, NQ)
         quantize(nc, y_codes[:, 0:HALF], y_scale[:, 0:HALF], y_woven[0][:, 0:HALF, :])
-        weave(nc.scalar.copy, y_woven[1][:, 0:TAIL, :], ys[1][:, :, 0:TAIL])
-        weave(nc.vector.tensor_copy, y_woven[1][:, TAIL:W, :], ys[1][:, :, TAIL:W])
+        weave(nc.scalar.copy, y_woven[1][:, HALF:W, :], ys[1][:, :, HALF:W])
+        weave(nc.vector.tensor_copy, y_woven[1][:, 0:HALF, :], ys[1][:, :, 0:HALF])
         quantize(nc, y_codes[:, HALF:W], y_scale[:, HALF:W], y_woven[0][:, HALF:W, :])
-        nc.sync.dma_start(y_words[:, cols[0]], y_codes[:, cols[0]].bitcast(I32))
-        quantize(nc, y_codes[:, cols[1]], y_scale[:, cols[1]], y_woven[1][:])
-        nc.sync.dma_start(y_words[:, cols[1]], y_codes[:, cols[1]].bitcast(I32))
+        quantize(nc, y_codes[:, third], y_scale[:, third], y_woven[1][:, 0:HALF, :])
+        nc.sync.dma_start(y_words[:, 0 : W + HALF], y_codes[:, 0 : W + HALF].bitcast(I32))
+        quantize(nc, y_codes[:, fourth], y_scale[:, fourth], y_woven[1][:, HALF:W, :])
+        nc.sync.dma_start(y_words[:, fourth], y_codes[:, fourth].bitcast(I32))
         for quad in range(4):
             queue = nc.scalar if quad % 2 == 0 else nc.sync
             queue.dma_start(

@@ -136,28 +136,35 @@ def tile_attend_plw_decay_srt_kernel(tc, qT, k_words, k_scales, dk, dc, offs, ou
         y_woven = [sb.tile([P, W, PACK], BF16, name="y_woven0", align_bytes=64), sb.tile([P, W, PACK], BF16, name="y_woven1", align_bytes=64)]
         bank_tags = [["bank_0", "bank_1", "bank_2", "bank_3"], ["bank_4", "bank_5", "bank_dk", "bank_dc"]]
         for c in range(CHUNKS):
-            scores = [ps.tile([P, W], F32, name=f"score{c}_{t}", tag=bank_tags[c][t]) for t in range(PACK)]
-            for t in range(PACK):
+            parts = [(t, slice(0, W), bank_tags[c][t]) for t in range(PACK)]
+            if c == CHUNKS - 1:
+                parts = parts[:-1] + [(PACK - 1, slice(HALF, W), "bank_dc"), (PACK - 1, slice(0, HALF), "bank_0")]
+            scores = []
+            for t, part, tag in parts:
+                score = ps.tile([P, part.stop - part.start], F32, name=f"score{c}_{t}_{part.start}", tag=tag)
+                scores.append(score)
                 nc.tensor.matmul_mx(
-                    out=scores[t][:],
+                    out=score[:],
                     lhsT=k_codes[:, t * P : (t + 1) * P].bitcast(FP8X4),
                     lhsT_scale=k_scale[:, t * P : (t + 1) * P],
-                    rhs=q_codes[c][:].bitcast(FP8X4),
-                    rhs_scale=q_scale[c][:],
+                    rhs=q_codes[c][:, part].bitcast(FP8X4),
+                    rhs_scale=q_scale[c][:, part],
                     start=True,
                     stop=True,
                 )
-            for t in range(PACK):
+            for score, (t, part, tag) in zip(scores, parts):
+                decay = dc_rows[:, cols[c]][:, part]
                 if c == 0 and t == 0:
                     scaled = placed([P, W], F32, f"scaled{c}", 18432 + 4 * W * c)
-                    nc.scalar.activation(scaled[:], scores[t][:], COPY, scale=dk_slots[:, t : t + 1])
-                    nc.gpsimd.tensor_tensor(ys[c][:, t, :], scaled[:], dc_rows[:, cols[c]], MULT)
+                    for half in (slice(0, HALF), slice(HALF, W)):
+                        nc.scalar.activation(scaled[:, half], score[:, half], COPY, scale=dk_slots[:, t : t + 1])
+                        nc.gpsimd.tensor_tensor(ys[c][:, t, half], scaled[:, half], decay[:, half], MULT)
                 else:
                     nc.vector.scalar_tensor_tensor(
-                        out=ys[c][:, t, :],
-                        in0=scores[t][:],
+                        out=ys[c][:, t, part],
+                        in0=score[:],
                         scalar=dk_slots[:, t : t + 1],
-                        in1=dc_rows[:, cols[c]],
+                        in1=decay,
                         op0=MULT,
                         op1=MULT,
                     )

@@ -23,8 +23,9 @@ W = 256
 HALF = W // 2
 CHUNKS = NQ // W
 SPLIT = 1088
+TAIL = 192
 STORES = (
-    (slice(1, 2), slice(2, 3), slice(0, 1), slice(3, 4)),
+    (slice(0, 1), slice(1, 2), slice(2, 3), slice(3, 4)),
     (slice(0, 2), slice(2, 4)),
 )
 REACH = T - N // 2
@@ -133,12 +134,14 @@ def tile_attend_plw_decay_srt_kernel(tc, qT, k_words, k_scales, dk, dc, offs, ou
         y_rows = out_0.rearrange("(p t) q -> p t q", t=PACK)
         y_words = out_1[0].rearrange("p q u -> p (q u)").bitcast(I32)
         ys = [placed([P, PACK, W], F32, "y0", 20480), sb.tile([P, PACK, W], F32, name="y1")]
-        y_woven = [sb.tile([P, W, PACK], BF16, name="y_woven0", align_bytes=64), sb.tile([P, W, PACK], BF16, name="y_woven1", align_bytes=64)]
+        y_woven = [sb.tile([P, HALF, PACK], BF16, name="y_woven0", align_bytes=64), sb.tile([P, W, PACK], BF16, name="y_woven1", align_bytes=64)]
+        y_side = sb.tile([P, HALF, PACK], BF16, name="y_side", align_bytes=64)
         bank_tags = [["bank_0", "bank_1", "bank_2", "bank_3"], ["bank_4", "bank_5", "bank_dk", "bank_dc"]]
         for c in range(CHUNKS):
             parts = [(t, slice(0, W), bank_tags[c][t]) for t in range(PACK)]
             if c == CHUNKS - 1:
-                parts = parts[:-1] + [(PACK - 1, slice(HALF, W), "bank_dc"), (PACK - 1, slice(0, HALF), "bank_0")]
+                left, right = slice(0, HALF), slice(HALF, W)
+                parts = parts[:2] + [(2, left, "bank_dk"), (3, left, "bank_dc"), (2, right, "bank_0"), (3, right, "bank_1")]
             scores = []
             for t, part, tag in parts:
                 score = ps.tile([P, part.stop - part.start], F32, name=f"score{c}_{t}_{part.start}", tag=tag)
@@ -154,23 +157,25 @@ def tile_attend_plw_decay_srt_kernel(tc, qT, k_words, k_scales, dk, dc, offs, ou
                 )
             for score, (t, part, tag) in zip(scores, parts):
                 decay = dc_rows[:, cols[c]][:, part]
-                if c == 0 and t == 0:
-                    scaled = placed([P, W], F32, f"scaled{c}", 18432 + 4 * W * c)
-                    for half in (slice(0, HALF), slice(HALF, W)):
-                        nc.scalar.activation(scaled[:, half], score[:, half], COPY, scale=dk_slots[:, t : t + 1])
-                        nc.gpsimd.tensor_tensor(ys[c][:, t, half], scaled[:, half], decay[:, half], MULT)
-                else:
-                    nc.vector.scalar_tensor_tensor(
-                        out=ys[c][:, t, part],
-                        in0=score[:],
-                        scalar=dk_slots[:, t : t + 1],
-                        in1=decay,
-                        op0=MULT,
-                        op1=MULT,
-                    )
+                nc.vector.scalar_tensor_tensor(
+                    out=ys[c][:, t, part],
+                    in0=score[:],
+                    scalar=dk_slots[:, t : t + 1],
+                    in1=decay,
+                    op0=MULT,
+                    op1=MULT,
+                )
             if c == 0:
                 weave(nc.scalar.copy, y_woven[0][:, 0:HALF, :], ys[0][:, :, 0:HALF])
-                weave(nc.scalar.copy, y_woven[0][:, HALF:W, :], ys[0][:, :, HALF:W])
+                weave(nc.scalar.copy, y_side[:, 0:64, :], ys[0][:, :, HALF : HALF + 64])
+                nc.gpsimd.tensor_scalar(
+                    y_side[:, 64:HALF, :].rearrange("p (c i) t -> p c t i", i=4),
+                    ys[0][:, :, HALF + 64 : W].rearrange("p t (c i) -> p c t i", i=4),
+                    1.0,
+                    0.0,
+                    MULT,
+                    mybir.AluOpType.add,
+                )
             for places in STORES[c]:
                 nc.sync.dma_start(y_rows[:, places, cols[c]], ys[c][:, places, :])
         y_codes = placed([P, NQ], U32, "y_codes", 8192)
@@ -178,9 +183,10 @@ def tile_attend_plw_decay_srt_kernel(tc, qT, k_words, k_scales, dk, dc, offs, ou
         third = slice(W, W + HALF)
         fourth = slice(W + HALF, NQ)
         quantize(nc, y_codes[:, 0:HALF], y_scale[:, 0:HALF], y_woven[0][:, 0:HALF, :])
-        weave(nc.scalar.copy, y_woven[1][:, HALF:W, :], ys[1][:, :, HALF:W])
-        weave(nc.vector.tensor_copy, y_woven[1][:, 0:HALF, :], ys[1][:, :, 0:HALF])
-        quantize(nc, y_codes[:, HALF:W], y_scale[:, HALF:W], y_woven[0][:, HALF:W, :])
+        weave(nc.scalar.copy, y_woven[1][:, 0:HALF, :], ys[1][:, :, 0:HALF])
+        weave(nc.scalar.copy, y_woven[1][:, HALF:TAIL, :], ys[1][:, :, HALF:TAIL])
+        weave(nc.vector.tensor_copy, y_woven[1][:, TAIL:W, :], ys[1][:, :, TAIL:W])
+        quantize(nc, y_codes[:, HALF:W], y_scale[:, HALF:W], y_side[:])
         quantize(nc, y_codes[:, third], y_scale[:, third], y_woven[1][:, 0:HALF, :])
         nc.sync.dma_start(y_words[:, 0 : W + HALF], y_codes[:, 0 : W + HALF].bitcast(I32))
         quantize(nc, y_codes[:, fourth], y_scale[:, fourth], y_woven[1][:, HALF:W, :])

@@ -11,7 +11,7 @@ U16 = mybir.dt.uint16
 U8 = mybir.dt.uint8
 FP8X4 = mybir.dt.float8_e4m3fn_x4
 MULT = mybir.AluOpType.mult
-COPY = mybir.ActivationFunctionType.Copy
+ADD = mybir.AluOpType.add
 
 P = 128
 PACK = 4
@@ -22,7 +22,10 @@ NQ = 512
 W = 256
 HALF = W // 2
 CHUNKS = NQ // W
+QUADS = 4
+SCALE_ROW = 48
 SPLIT = 1088
+SIDE = 64
 TAIL = 192
 STORES = (
     (slice(0, 1), slice(1, 2), slice(2, 3), slice(3, 4)),
@@ -30,15 +33,30 @@ STORES = (
 )
 REACH = T - N // 2
 
+AT_Q_RAW = (0, 18432)
+AT_DK_SLOTS = 512
+AT_Q_WOVEN = 4096
+AT_IDENT = 6144
+AT_CODES = (8192, 9216)
+AT_WORDS = 10240
+AT_Y_FIRST = 20480
+AT_DC_ROWS = 24576
+AT_SCALES = 28672
+
 FLOPS = 2 * N * D * NQ
 BYTES = 4 * D * NQ + D * T + 16 * T + 4 * T + 4 * NQ + 2 * P * N // 16 + 4 * N * NQ + N * NQ + 16 * NQ
 
 
+def woven_walk(dst):
+    return dst.rearrange("p (c i) t -> p c t i", i=4)
+
+
+def rows_walk(src):
+    return src.rearrange("p t (c i) -> p c t i", i=4)
+
+
 def weave(copy, dst, src):
-    copy(
-        out=dst.rearrange("p (c i) t -> p c t i", i=4),
-        in_=src.rearrange("p t (c i) -> p c t i", i=4),
-    )
+    copy(out=woven_walk(dst), in_=rows_walk(src))
 
 
 def quantize(nc, codes, scales, woven):
@@ -58,15 +76,15 @@ def tile_attend_plw_decay_srt_kernel(tc, qT, k_words, k_scales, dk, dc, offs, ou
 
         offsets = sb.tile([P, N // 16], U16, name="offsets")
         dk_pool = sb.tile([P, T], F32, name="dk_pool")
-        word_pool = placed([P, T], U32, "word_pool", 10240)
-        scale_pool = placed([P, T], U8, "scale_pool", 28672)
-        ident = placed([P, P], F32, "ident", 6144)
+        word_pool = placed([P, T], U32, "word_pool", AT_WORDS)
+        scale_pool = placed([P, T], U8, "scale_pool", AT_SCALES)
+        ident = placed([P, P], F32, "ident", AT_IDENT)
         dc_quads = sb.tile([P, PACK], F32, name="dc_quads")
-        q_raw = [placed([P, PACK, W], F32, "q_raw0", 0), placed([P, PACK, W], F32, "q_raw1", 18432)]
+        q_raw = [placed([P, PACK, W], F32, f"q_raw{c}", AT_Q_RAW[c]) for c in range(CHUNKS)]
 
         scale_zero = scale_pool[:].bitcast(I32)
-        nc.gpsimd.memset(scale_zero[0:48, :], 0)
-        nc.gpsimd.memset(scale_zero[64:P, :], 0)
+        nc.gpsimd.memset(scale_zero[0:SCALE_ROW, :], 0)
+        nc.gpsimd.memset(scale_zero[SCALE_ROW + 16 : P, :], 0)
         make_identity(nc, ident[:])
         dk_zero = dk_pool[0 : P - 1, :].bitcast(I32)
         nc.vector.memset(dk_zero[:, 0 : SPLIT - 1], 0)
@@ -75,7 +93,7 @@ def tile_attend_plw_decay_srt_kernel(tc, qT, k_words, k_scales, dk, dc, offs, ou
 
         q_rows = qT[0].rearrange("(p t) q -> p t q", t=PACK)
         nc.sync.dma_start(offsets[:], offs)
-        nc.sync.dma_start(scale_pool[48:64, :].bitcast(I32), k_scales[0].bitcast(I32))
+        nc.sync.dma_start(scale_pool[SCALE_ROW : SCALE_ROW + 16, :].bitcast(I32), k_scales[0].bitcast(I32))
         nc.sync.dma_start(dk_pool[P - 1 : P, :], dk[0:1, :])
         nc.sync.dma_start(q_raw[0][:], q_rows[:, :, cols[0]])
         nc.sync.dma_start(dc_quads[:], dc[0, 0].rearrange("(p u) -> p u", u=PACK))
@@ -91,19 +109,19 @@ def tile_attend_plw_decay_srt_kernel(tc, qT, k_words, k_scales, dk, dc, offs, ou
             k_scale[:].rearrange("p (t m) -> p t m", t=PACK),
             scale_listed[:].rearrange("p (m t) -> p t m", t=PACK),
         )
-        for quad in range(4):
+        for quad in range(QUADS):
             nc.sync.dma_start(
                 k_scale[32 * quad : 32 * quad + 4, :].bitcast(I32),
-                k_scale[48 + 4 * quad : 52 + 4 * quad, :].bitcast(I32),
+                k_scale[SCALE_ROW + 4 * quad : SCALE_ROW + 4 * quad + 4, :].bitcast(I32),
             )
-        dk_listed = placed([P, N], F32, "dk_listed", 28672)
+        dk_listed = placed([P, N], F32, "dk_listed", AT_SCALES)
         nc.vector.tensor_copy(dk_listed[:], dk_pool[:].indirect(offsets[:]))
 
-        q_woven = [placed([P, W, PACK], BF16, "q_woven0", 4096)]
-        q_codes = [placed([P, W], U32, "q_codes0", 8192)]
+        q_woven = placed([P, W, PACK], BF16, "q_woven0", AT_Q_WOVEN)
+        q_codes = [placed([P, W], U32, "q_codes0", AT_CODES[0])]
         q_scale = [sb.tile([P, W], U8, name=f"q_scale{c}", align_bytes=64) for c in range(CHUNKS)]
-        weave(nc.scalar.copy, q_woven[0][:], q_raw[0][:])
-        quantize(nc, q_codes[0][:], q_scale[0][:], q_woven[0][:])
+        weave(nc.scalar.copy, q_woven[:], q_raw[0][:])
+        quantize(nc, q_codes[0][:], q_scale[0][:], q_woven[:])
 
         k_codes = sb.tile([P, N], U32, name="k_codes", align_bytes=64)
         codes_dealt = k_codes[:].rearrange("p (t m) -> p m t", t=PACK)
@@ -113,35 +131,36 @@ def tile_attend_plw_decay_srt_kernel(tc, qT, k_words, k_scales, dk, dc, offs, ou
         dc_bank = ps.tile([P, PACK, P], F32, name="dc_bank", tag="bank_dc")
         for u in range(PACK):
             nc.tensor.transpose(dc_bank[:, u, :], dc_quads[:, u : u + 1].to_broadcast([P, P]), ident[:])
-        dc_rows = placed([P, NQ], F32, "dc_rows", 24576)
+        dc_rows = placed([P, NQ], F32, "dc_rows", AT_DC_ROWS)
         nc.scalar.copy(dc_rows[:].rearrange("p (n u) -> p n u", u=PACK), dc_bank[:].rearrange("p u n -> p n u"))
 
         dk_bank = ps.tile([P, PACK, P], F32, name="dk_bank", tag="bank_dk")
         dk_dealt = dk_listed[:].rearrange("p (m t) -> p t m", t=PACK)
         for t in range(PACK):
             nc.tensor.transpose(dk_bank[:, t, :], dk_dealt[:, t, :], ident[:])
-        dk_slots = placed([P, PACK], F32, "dk_slots", 512)
+        dk_slots = placed([P, PACK], F32, "dk_slots", AT_DK_SLOTS)
         nc.scalar.copy(dk_slots[:], dk_bank[:, :, P - 1])
 
-        q_left = placed([P, HALF, PACK], BF16, "q_left", 6144)
+        q_left = placed([P, HALF, PACK], BF16, "q_left", AT_IDENT)
         q_right = sb.tile([P, HALF, PACK], BF16, name="q_right", align_bytes=64)
         weave(nc.scalar.copy, q_left[:], q_raw[1][:, :, 0:HALF])
         weave(nc.vector.tensor_copy, q_right[:], q_raw[1][:, :, HALF:W])
-        q_codes.append(placed([P, W], U32, "q_codes1", 9216))
+        q_codes.append(placed([P, W], U32, "q_codes1", AT_CODES[1]))
         quantize(nc, q_codes[1][:, 0:HALF], q_scale[1][:, 0:HALF], q_left[:])
         quantize(nc, q_codes[1][:, HALF:W], q_scale[1][:, HALF:W], q_right[:])
 
         y_rows = out_0.rearrange("(p t) q -> p t q", t=PACK)
         y_words = out_1[0].rearrange("p q u -> p (q u)").bitcast(I32)
-        ys = [placed([P, PACK, W], F32, "y0", 20480), sb.tile([P, PACK, W], F32, name="y1")]
-        y_woven = [sb.tile([P, HALF, PACK], BF16, name="y_woven0", align_bytes=64), sb.tile([P, W, PACK], BF16, name="y_woven1", align_bytes=64)]
-        y_side = sb.tile([P, HALF, PACK], BF16, name="y_side", align_bytes=64)
-        bank_tags = [["bank_0", "bank_1", "bank_2", "bank_3"], ["bank_4", "bank_5", "bank_dk", "bank_dc"]]
-        for c in range(CHUNKS):
-            parts = [(t, slice(0, W), bank_tags[c][t]) for t in range(PACK)]
-            if c == CHUNKS - 1:
-                left, right = slice(0, HALF), slice(HALF, W)
-                parts = parts[:2] + [(2, left, "bank_dk"), (3, left, "bank_dc"), (2, right, "bank_0"), (3, right, "bank_1")]
+        ys = [placed([P, PACK, W], F32, "y0", AT_Y_FIRST), sb.tile([P, PACK, W], F32, name="y1")]
+        woven_first = sb.tile([P, HALF, PACK], BF16, name="y_woven0", align_bytes=64)
+        woven_last = sb.tile([P, W, PACK], BF16, name="y_woven1", align_bytes=64)
+        woven_second = sb.tile([P, HALF, PACK], BF16, name="y_side", align_bytes=64)
+        whole, left, right = slice(0, W), slice(0, HALF), slice(HALF, W)
+        chunk_parts = [
+            [(t, whole, f"bank_{t}") for t in range(PACK)],
+            [(0, whole, "bank_4"), (1, whole, "bank_5"), (2, left, "bank_dk"), (3, left, "bank_dc"), (2, right, "bank_0"), (3, right, "bank_1")],
+        ]
+        for c, parts in enumerate(chunk_parts):
             scores = []
             for t, part, tag in parts:
                 score = ps.tile([P, part.stop - part.start], F32, name=f"score{c}_{t}_{part.start}", tag=tag)
@@ -156,42 +175,42 @@ def tile_attend_plw_decay_srt_kernel(tc, qT, k_words, k_scales, dk, dc, offs, ou
                     stop=True,
                 )
             for score, (t, part, tag) in zip(scores, parts):
-                decay = dc_rows[:, cols[c]][:, part]
                 nc.vector.scalar_tensor_tensor(
                     out=ys[c][:, t, part],
                     in0=score[:],
                     scalar=dk_slots[:, t : t + 1],
-                    in1=decay,
+                    in1=dc_rows[:, cols[c]][:, part],
                     op0=MULT,
                     op1=MULT,
                 )
             if c == 0:
-                weave(nc.scalar.copy, y_woven[0][:, 0:HALF, :], ys[0][:, :, 0:HALF])
-                weave(nc.scalar.copy, y_side[:, 0:64, :], ys[0][:, :, HALF : HALF + 64])
+                weave(nc.scalar.copy, woven_first[:, left, :], ys[0][:, :, left])
+                weave(nc.scalar.copy, woven_second[:, 0:SIDE, :], ys[0][:, :, HALF : HALF + SIDE])
                 nc.gpsimd.tensor_scalar(
-                    y_side[:, 64:HALF, :].rearrange("p (c i) t -> p c t i", i=4),
-                    ys[0][:, :, HALF + 64 : W].rearrange("p t (c i) -> p c t i", i=4),
+                    woven_walk(woven_second[:, SIDE:HALF, :]),
+                    rows_walk(ys[0][:, :, HALF + SIDE : W]),
                     1.0,
-                    0.0,
+                    -0.0,
                     MULT,
-                    mybir.AluOpType.add,
+                    ADD,
                 )
             for places in STORES[c]:
                 nc.sync.dma_start(y_rows[:, places, cols[c]], ys[c][:, places, :])
-        y_codes = placed([P, NQ], U32, "y_codes", 8192)
+
+        y_codes = placed([P, NQ], U32, "y_codes", AT_CODES[0])
         y_scale = sb.tile([P, NQ], U8, name="y_scale", align_bytes=64)
         third = slice(W, W + HALF)
         fourth = slice(W + HALF, NQ)
-        quantize(nc, y_codes[:, 0:HALF], y_scale[:, 0:HALF], y_woven[0][:, 0:HALF, :])
-        weave(nc.scalar.copy, y_woven[1][:, 0:HALF, :], ys[1][:, :, 0:HALF])
-        weave(nc.scalar.copy, y_woven[1][:, HALF:TAIL, :], ys[1][:, :, HALF:TAIL])
-        weave(nc.vector.tensor_copy, y_woven[1][:, TAIL:W, :], ys[1][:, :, TAIL:W])
-        quantize(nc, y_codes[:, HALF:W], y_scale[:, HALF:W], y_side[:])
-        quantize(nc, y_codes[:, third], y_scale[:, third], y_woven[1][:, 0:HALF, :])
+        quantize(nc, y_codes[:, left], y_scale[:, left], woven_first[:, left, :])
+        weave(nc.scalar.copy, woven_last[:, left, :], ys[1][:, :, left])
+        weave(nc.scalar.copy, woven_last[:, HALF:TAIL, :], ys[1][:, :, HALF:TAIL])
+        weave(nc.vector.tensor_copy, woven_last[:, TAIL:W, :], ys[1][:, :, TAIL:W])
+        quantize(nc, y_codes[:, right], y_scale[:, right], woven_second[:])
+        quantize(nc, y_codes[:, third], y_scale[:, third], woven_last[:, left, :])
         nc.sync.dma_start(y_words[:, 0 : W + HALF], y_codes[:, 0 : W + HALF].bitcast(I32))
-        quantize(nc, y_codes[:, fourth], y_scale[:, fourth], y_woven[1][:, HALF:W, :])
+        quantize(nc, y_codes[:, fourth], y_scale[:, fourth], woven_last[:, right, :])
         nc.sync.dma_start(y_words[:, fourth], y_codes[:, fourth].bitcast(I32))
-        for quad in range(4):
+        for quad in range(QUADS):
             queue = nc.scalar if quad % 2 == 0 else nc.sync
             queue.dma_start(
                 out_2[0, 4 * quad : 4 * quad + 4, :].bitcast(I32),

@@ -90,6 +90,8 @@ def tile_attend_plw_decay_srt_kernel(tc, qT, k_words, k_scales, dk, dc, offs, ou
         nc.vector.memset(dk_zero[:, 0 : SPLIT - 1], 0)
         nc.vector.memset(dk_zero[:, SPLIT - 1 : SPLIT], 0)
         nc.gpsimd.memset(dk_zero[:, SPLIT:T], 0)
+        k_scale = sb.tile([P, N], U8, name="k_scale", align_bytes=64)
+        nc.vector.memset(k_scale[:].bitcast(I32), 0)
 
         q_rows = qT[0].rearrange("(p t) q -> p t q", t=PACK)
         nc.sync.dma_start(offsets[:], offs)
@@ -103,16 +105,11 @@ def tile_attend_plw_decay_srt_kernel(tc, qT, k_words, k_scales, dk, dc, offs, ou
         nc.sync.dma_start(q_raw[1][:], q_rows[:, :, cols[1]])
 
         scale_listed = sb.tile([P, N], U8, name="scale_listed")
-        nc.vector.tensor_copy(scale_listed[:], scale_pool[:].indirect(offsets[:]))
-        k_scale = sb.tile([P, N], U8, name="k_scale", align_bytes=64)
-        nc.vector.tensor_copy(
-            k_scale[:].rearrange("p (t m) -> p t m", t=PACK),
-            scale_listed[:].rearrange("p (m t) -> p t m", t=PACK),
-        )
+        nc.vector.tensor_copy(scale_listed[:].rearrange("p (t m) -> p m t", t=PACK), scale_pool[:].indirect(offsets[:]))
         for quad in range(QUADS):
             nc.sync.dma_start(
                 k_scale[32 * quad : 32 * quad + 4, :].bitcast(I32),
-                k_scale[SCALE_ROW + 4 * quad : SCALE_ROW + 4 * quad + 4, :].bitcast(I32),
+                scale_listed[SCALE_ROW + 4 * quad : SCALE_ROW + 4 * quad + 4, :].bitcast(I32),
             )
         dk_listed = placed([P, N], F32, "dk_listed", AT_SCALES)
         nc.vector.tensor_copy(dk_listed[:], dk_pool[:].indirect(offsets[:]))

@@ -203,10 +203,10 @@ def tile_attend_plw_decay_srt_kernel(tc, qT, k_words, k_scales, dk, dc, offs, ou
         weave(nc.scalar.copy, woven_last[:, HALF:TAIL, :], ys[1][:, :, HALF:TAIL])
         weave(nc.vector.tensor_copy, woven_last[:, TAIL:W, :], ys[1][:, :, TAIL:W])
         quantize(nc, y_codes[:, right], y_scale[:, right], woven_second[:])
+        nc.sync.dma_start(y_words[:, cols[0]], y_codes[:, cols[0]].bitcast(I32))
         quantize(nc, y_codes[:, third], y_scale[:, third], woven_last[:, left, :])
-        nc.sync.dma_start(y_words[:, 0 : W + HALF], y_codes[:, 0 : W + HALF].bitcast(I32))
         quantize(nc, y_codes[:, fourth], y_scale[:, fourth], woven_last[:, right, :])
-        nc.sync.dma_start(y_words[:, fourth], y_codes[:, fourth].bitcast(I32))
+        nc.sync.dma_start(y_words[:, cols[1]], y_codes[:, cols[1]].bitcast(I32))
         for quad in range(QUADS):
             queue = nc.scalar if quad % 2 == 0 else nc.sync
             queue.dma_start(

@@ -22,6 +22,8 @@ NQ = 512
 W = 256
 HALF = W // 2
 CHUNKS = NQ // W
+DC_ROWS = 64
+DC_RUN = NQ // DC_ROWS
 QUADS = 4
 SCALE_ROW = 48
 SPLIT = 1088
@@ -79,7 +81,7 @@ def tile_attend_plw_decay_srt_kernel(tc, qT, k_words, k_scales, dk, dc, offs, ou
         word_pool = placed([P, T], U32, "word_pool", AT_WORDS)
         scale_pool = placed([P, T], U8, "scale_pool", AT_SCALES)
         ident = placed([P, P], F32, "ident", AT_IDENT)
-        dc_quads = sb.tile([P, PACK], F32, name="dc_quads")
+        dc_runs = sb.tile([P, DC_RUN], F32, name="dc_runs")
         q_raw = [placed([P, PACK, W], F32, f"q_raw{c}", AT_Q_RAW[c]) for c in range(CHUNKS)]
 
         scale_zero = scale_pool[:].bitcast(I32)
@@ -92,13 +94,14 @@ def tile_attend_plw_decay_srt_kernel(tc, qT, k_words, k_scales, dk, dc, offs, ou
         nc.gpsimd.memset(dk_zero[:, SPLIT:T], 0)
         k_scale = sb.tile([P, N], U8, name="k_scale", align_bytes=64)
         nc.vector.memset(k_scale[:].bitcast(I32), 0)
+        nc.vector.memset(dc_runs[DC_ROWS:P, :], 0.0)
 
         q_rows = qT[0].rearrange("(p t) q -> p t q", t=PACK)
         nc.sync.dma_start(offsets[:], offs)
         nc.sync.dma_start(scale_pool[SCALE_ROW : SCALE_ROW + 16, :].bitcast(I32), k_scales[0].bitcast(I32))
         nc.sync.dma_start(dk_pool[P - 1 : P, :], dk[0:1, :])
         nc.sync.dma_start(q_raw[0][:], q_rows[:, :, cols[0]])
-        nc.sync.dma_start(dc_quads[:], dc[0, 0].rearrange("(p u) -> p u", u=PACK))
+        nc.sync.dma_start(dc_runs[0:DC_ROWS, :], dc[0, 0].rearrange("(p u) -> p u", u=DC_RUN))
         word_rows = k_words[0].rearrange("p n r -> p (n r)").bitcast(I32)
         nc.sync.dma_start(word_pool[:, 0:REACH].bitcast(I32), word_rows[:, 0:REACH])
         nc.sync.dma_start(word_pool[:, REACH:T].bitcast(I32), word_rows[:, REACH:T])
@@ -125,11 +128,13 @@ def tile_attend_plw_decay_srt_kernel(tc, qT, k_words, k_scales, dk, dc, offs, ou
         nc.vector.tensor_copy(codes_dealt[:, 0 : P // 2, :], word_pool[:, 0:REACH].indirect(offsets[:, 0 : N // 32]))
         nc.vector.tensor_copy(codes_dealt[:, P // 2 : P, :], word_pool[:].indirect(offsets[:, N // 32 : N // 16]))
 
-        dc_bank = ps.tile([P, PACK, P], F32, name="dc_bank", tag="bank_dc")
-        for u in range(PACK):
-            nc.tensor.transpose(dc_bank[:, u, :], dc_quads[:, u : u + 1].to_broadcast([P, P]), ident[:])
         dc_rows = placed([P, NQ], F32, "dc_rows", AT_DC_ROWS)
-        nc.scalar.copy(dc_rows[:].rearrange("p (n u) -> p n u", u=PACK), dc_bank[:].rearrange("p u n -> p n u"))
+        dc_by_run = dc_rows[:].rearrange("p (n u) -> p n u", u=DC_RUN)
+        for first, tag in ((0, "bank_dc"), (PACK, "bank_5")):
+            dc_bank = ps.tile([P, PACK, P], F32, name=f"dc_bank{first}", tag=tag)
+            for u in range(PACK):
+                nc.tensor.transpose(dc_bank[:, u, :], dc_runs[:, first + u : first + u + 1].to_broadcast([P, P]), ident[:])
+            nc.scalar.copy(dc_by_run[:, :, first : first + PACK], dc_bank[:, :, 0:DC_ROWS].rearrange("p u n -> p n u"))
 
         dk_bank = ps.tile([P, PACK, P], F32, name="dk_bank", tag="bank_dk")
         dk_dealt = dk_listed[:].rearrange("p (m t) -> p t m", t=PACK)

@@ -27,8 +27,8 @@ DC_RUN = NQ // DC_ROWS
 QUADS = 4
 SCALE_ROW = 48
 SPLIT = 1088
-SIDE = 64
-TAIL = 192
+SIDE = 48
+TAIL = 176
 STORES = (
     (slice(0, 1), slice(1, 2), slice(2, 3), slice(3, 4)),
     (slice(0, 2), slice(2, 4)),

from contextlib import ExitStack

import concourse.mybir as mybir
from concourse.masks import make_identity

F32 = mybir.dt.float32
BF16 = mybir.dt.bfloat16
I32 = mybir.dt.int32
U32 = mybir.dt.uint32
U16 = mybir.dt.uint16
U8 = mybir.dt.uint8
FP8X4 = mybir.dt.float8_e4m3fn_x4
MULT = mybir.AluOpType.mult
ADD = mybir.AluOpType.add

P = 128
PACK = 4
T = 2048
N = 512
D = 512
NQ = 512
W = 256
HALF = W // 2
CHUNKS = NQ // W
DC_ROWS = 64
DC_RUN = NQ // DC_ROWS
QUADS = 4
SCALE_ROW = 48
SPLIT = 1088
SIDE = 48
TAIL = 176
STORES = (
    (slice(0, 1), slice(1, 2), slice(2, 3), slice(3, 4)),
    (slice(0, 2), slice(2, 4)),
)
REACH = T - N // 2

AT_Q_RAW = (0, 18432)
AT_DK_SLOTS = 512
AT_Q_WOVEN = 4096
AT_IDENT = 6144
AT_CODES = (8192, 9216)
AT_WORDS = 10240
AT_Y_FIRST = 20480
AT_DC_ROWS = 24576
AT_SCALES = 28672

FLOPS = 2 * N * D * NQ
BYTES = 4 * D * NQ + D * T + 16 * T + 4 * T + 4 * NQ + 2 * P * N // 16 + 4 * N * NQ + N * NQ + 16 * NQ


def woven_walk(dst):
    return dst.rearrange("p (c i) t -> p c t i", i=4)


def rows_walk(src):
    return src.rearrange("p t (c i) -> p c t i", i=4)


def weave(copy, dst, src):
    copy(out=woven_walk(dst), in_=rows_walk(src))


def quantize(nc, codes, scales, woven):
    nc.vector.quantize_mx(out=codes.bitcast(FP8X4), scales=scales, in_=woven.rearrange("p w t -> p (w t)"))


def tile_attend_plw_decay_srt_kernel(tc, qT, k_words, k_scales, dk, dc, offs, out_0, out_1, out_2):
    nc = tc.nc
    cols = [slice(c * W, (c + 1) * W) for c in range(CHUNKS)]
    with ExitStack() as ctx:
        sb = ctx.enter_context(tc.tile_pool(name="sb", bufs=1))
        shared = ctx.enter_context(tc.tile_pool(name="shared", bufs=1))
        ps = ctx.enter_context(tc.psum_pool(name="ps", bufs=1))

        def placed(shape, dtype, name, offset):
            return shared.tile(shape, dtype, name=name, offset=offset, align_bytes=64)

        offsets = sb.tile([P, N // 16], U16, name="offsets")
        dk_pool = sb.tile([P, T], F32, name="dk_pool")
        word_pool = placed([P, T], U32, "word_pool", AT_WORDS)
        scale_pool = placed([P, T], U8, "scale_pool", AT_SCALES)
        ident = placed([P, P], F32, "ident", AT_IDENT)
        dc_runs = sb.tile([P, DC_RUN], F32, name="dc_runs")
        q_raw = [placed([P, PACK, W], F32, f"q_raw{c}", AT_Q_RAW[c]) for c in range(CHUNKS)]

        scale_zero = scale_pool[:].bitcast(I32)
        nc.gpsimd.memset(scale_zero[0:SCALE_ROW, :], 0)
        nc.gpsimd.memset(scale_zero[SCALE_ROW + 16 : P, :], 0)
        make_identity(nc, ident[:])
        dk_zero = dk_pool[0 : P - 1, :].bitcast(I32)
        nc.vector.memset(dk_zero[:, 0 : SPLIT - 1], 0)
        nc.vector.memset(dk_zero[:, SPLIT - 1 : SPLIT], 0)
        nc.gpsimd.memset(dk_zero[:, SPLIT:T], 0)
        k_scale = sb.tile([P, N], U8, name="k_scale", align_bytes=64)
        nc.vector.memset(k_scale[:].bitcast(I32), 0)
        nc.vector.memset(dc_runs[DC_ROWS:P, :], 0.0)

        q_rows = qT[0].rearrange("(p t) q -> p t q", t=PACK)
        nc.sync.dma_start(offsets[:], offs)
        nc.sync.dma_start(scale_pool[SCALE_ROW : SCALE_ROW + 16, :].bitcast(I32), k_scales[0].bitcast(I32))
        nc.sync.dma_start(dk_pool[P - 1 : P, :], dk[0:1, :])
        nc.sync.dma_start(q_raw[0][:], q_rows[:, :, cols[0]])
        nc.sync.dma_start(dc_runs[0:DC_ROWS, :], dc[0, 0].rearrange("(p u) -> p u", u=DC_RUN))
        word_rows = k_words[0].rearrange("p n r -> p (n r)").bitcast(I32)
        nc.sync.dma_start(word_pool[:, 0:REACH].bitcast(I32), word_rows[:, 0:REACH])
        nc.sync.dma_start(word_pool[:, REACH:T].bitcast(I32), word_rows[:, REACH:T])
        nc.sync.dma_start(q_raw[1][:], q_rows[:, :, cols[1]])

        scale_listed = sb.tile([P, N], U8, name="scale_listed")
        nc.vector.tensor_copy(scale_listed[:].rearrange("p (t m) -> p m t", t=PACK), scale_pool[:].indirect(offsets[:]))
        for quad in range(QUADS):
            nc.sync.dma_start(
                k_scale[32 * quad : 32 * quad + 4, :].bitcast(I32),
                scale_listed[SCALE_ROW + 4 * quad : SCALE_ROW + 4 * quad + 4, :].bitcast(I32),
            )
        dk_listed = placed([P, N], F32, "dk_listed", AT_SCALES)
        nc.vector.tensor_copy(dk_listed[:], dk_pool[:].indirect(offsets[:]))

        q_woven = placed([P, W, PACK], BF16, "q_woven0", AT_Q_WOVEN)
        q_codes = [placed([P, W], U32, "q_codes0", AT_CODES[0])]
        q_scale = [sb.tile([P, W], U8, name=f"q_scale{c}", align_bytes=64) for c in range(CHUNKS)]
        weave(nc.scalar.copy, q_woven[:], q_raw[0][:])
        quantize(nc, q_codes[0][:], q_scale[0][:], q_woven[:])

        k_codes = sb.tile([P, N], U32, name="k_codes", align_bytes=64)
        codes_dealt = k_codes[:].rearrange("p (t m) -> p m t", t=PACK)
        nc.vector.tensor_copy(codes_dealt[:, 0 : P // 2, :], word_pool[:, 0:REACH].indirect(offsets[:, 0 : N // 32]))
        nc.vector.tensor_copy(codes_dealt[:, P // 2 : P, :], word_pool[:].indirect(offsets[:, N // 32 : N // 16]))

        dc_rows = placed([P, NQ], F32, "dc_rows", AT_DC_ROWS)
        dc_by_run = dc_rows[:].rearrange("p (n u) -> p n u", u=DC_RUN)
        for first, tag in ((0, "bank_dc"), (PACK, "bank_5")):
            dc_bank = ps.tile([P, PACK, P], F32, name=f"dc_bank{first}", tag=tag)
            for u in range(PACK):
                nc.tensor.transpose(dc_bank[:, u, :], dc_runs[:, first + u : first + u + 1].to_broadcast([P, P]), ident[:])
            nc.scalar.copy(dc_by_run[:, :, first : first + PACK], dc_bank[:, :, 0:DC_ROWS].rearrange("p u n -> p n u"))

        dk_bank = ps.tile([P, PACK, P], F32, name="dk_bank", tag="bank_dk")
        dk_dealt = dk_listed[:].rearrange("p (m t) -> p t m", t=PACK)
        for t in range(PACK):
            nc.tensor.transpose(dk_bank[:, t, :], dk_dealt[:, t, :], ident[:])
        dk_slots = placed([P, PACK], F32, "dk_slots", AT_DK_SLOTS)
        nc.scalar.copy(dk_slots[:], dk_bank[:, :, P - 1])

        q_left = placed([P, HALF, PACK], BF16, "q_left", AT_IDENT)
        q_right = sb.tile([P, HALF, PACK], BF16, name="q_right", align_bytes=64)
        weave(nc.scalar.copy, q_left[:], q_raw[1][:, :, 0:HALF])
        weave(nc.vector.tensor_copy, q_right[:], q_raw[1][:, :, HALF:W])
        q_codes.append(placed([P, W], U32, "q_codes1", AT_CODES[1]))
        quantize(nc, q_codes[1][:, 0:HALF], q_scale[1][:, 0:HALF], q_left[:])
        quantize(nc, q_codes[1][:, HALF:W], q_scale[1][:, HALF:W], q_right[:])

        y_rows = out_0.rearrange("(p t) q -> p t q", t=PACK)
        y_words = out_1[0].rearrange("p q u -> p (q u)").bitcast(I32)
        ys = [placed([P, PACK, W], F32, "y0", AT_Y_FIRST), sb.tile([P, PACK, W], F32, name="y1")]
        woven_first = sb.tile([P, HALF, PACK], BF16, name="y_woven0", align_bytes=64)
        woven_last = sb.tile([P, W, PACK], BF16, name="y_woven1", align_bytes=64)
        woven_second = sb.tile([P, HALF, PACK], BF16, name="y_side", align_bytes=64)
        whole, left, right = slice(0, W), slice(0, HALF), slice(HALF, W)
        chunk_parts = [
            [(t, whole, f"bank_{t}") for t in range(PACK)],
            [(0, whole, "bank_4"), (1, whole, "bank_5"), (2, left, "bank_dk"), (3, left, "bank_dc"), (2, right, "bank_0"), (3, right, "bank_1")],
        ]
        for c, parts in enumerate(chunk_parts):
            scores = []
            for t, part, tag in parts:
                score = ps.tile([P, part.stop - part.start], F32, name=f"score{c}_{t}_{part.start}", tag=tag)
                scores.append(score)
                nc.tensor.matmul_mx(
                    out=score[:],
                    lhsT=k_codes[:, t * P : (t + 1) * P].bitcast(FP8X4),
                    lhsT_scale=k_scale[:, t * P : (t + 1) * P],
                    rhs=q_codes[c][:, part].bitcast(FP8X4),
                    rhs_scale=q_scale[c][:, part],
                    start=True,
                    stop=True,
                )
            for score, (t, part, tag) in zip(scores, parts):
                nc.vector.scalar_tensor_tensor(
                    out=ys[c][:, t, part],
                    in0=score[:],
                    scalar=dk_slots[:, t : t + 1],
                    in1=dc_rows[:, cols[c]][:, part],
                    op0=MULT,
                    op1=MULT,
                )
            if c == 0:
                weave(nc.scalar.copy, woven_first[:, left, :], ys[0][:, :, left])
                weave(nc.scalar.copy, woven_second[:, 0:SIDE, :], ys[0][:, :, HALF : HALF + SIDE])
                nc.gpsimd.tensor_scalar(
                    woven_walk(woven_second[:, SIDE:HALF, :]),
                    rows_walk(ys[0][:, :, HALF + SIDE : W]),
                    1.0,
                    -0.0,
                    MULT,
                    ADD,
                )
            for places in STORES[c]:
                nc.sync.dma_start(y_rows[:, places, cols[c]], ys[c][:, places, :])

        y_codes = placed([P, NQ], U32, "y_codes", AT_CODES[0])
        y_scale = sb.tile([P, NQ], U8, name="y_scale", align_bytes=64)
        third = slice(W, W + HALF)
        fourth = slice(W + HALF, NQ)
        quantize(nc, y_codes[:, left], y_scale[:, left], woven_first[:, left, :])
        weave(nc.scalar.copy, woven_last[:, left, :], ys[1][:, :, left])
        weave(nc.scalar.copy, woven_last[:, HALF:TAIL, :], ys[1][:, :, HALF:TAIL])
        weave(nc.vector.tensor_copy, woven_last[:, TAIL:W, :], ys[1][:, :, TAIL:W])
        quantize(nc, y_codes[:, right], y_scale[:, right], woven_second[:])
        nc.sync.dma_start(y_words[:, cols[0]], y_codes[:, cols[0]].bitcast(I32))
        quantize(nc, y_codes[:, third], y_scale[:, third], woven_last[:, left, :])
        quantize(nc, y_codes[:, fourth], y_scale[:, fourth], woven_last[:, right, :])
        nc.sync.dma_start(y_words[:, cols[1]], y_codes[:, cols[1]].bitcast(I32))
        for quad in range(QUADS):
            queue = nc.scalar if quad % 2 == 0 else nc.sync
            queue.dma_start(
                out_2[0, 4 * quad : 4 * quad + 4, :].bitcast(I32),
                y_scale[32 * quad : 32 * quad + 4, :].bitcast(I32),
            )
